import numpy as np, ml_dtypes
CORES = [36,164,52,180,100,228,116,244]
N = 8
BF = ml_dtypes.bfloat16
W, I, C, V, ST = 2048, 128, 512, 5, 1
def legs(v):
    return np.ascontiguousarray(np.swapaxes(v.reshape(N, 8, 16, I), 2, 3)).astype(np.int32)
def unlegs(v):
    return np.ascontiguousarray(np.swapaxes(v, 2, 3)).reshape(N, 128, I)
def spot(n, al):
    return (((n * (2 * al + 1)) >> 3) + n + 37 * al) & (W - 1)
def pick(x, ix):
    return np.take_along_axis(x, ix.reshape(N, 8, 1, I * 16), 3).reshape(N, 8, 16, I, 16)
def look(x, s, e, l, t, a, b, am):
    run = np.add.accumulate(t, axis=3); tot = run[..., 15:]
    al = (a[..., None] + run) & 255
    be = (b[..., None] + am[:, None, None, None] - (tot - run)) & 255
    f = pick(x, spot(l, al)); g = pick(x, spot(l, be))
    p = s[..., None] + np.add.accumulate(f, axis=4) - f
    q = e[..., None] - (np.add.reduce(g, axis=4, keepdims=True) - np.add.accumulate(g, axis=4) + g)
    d = np.add.reduce(np.minimum(np.abs(p - q), 255), axis=2)
    return f, g, p, tot, d
def parts(rng):
    x = rng.integers(0, 16, (N, 8, 16, W), dtype=np.int32); l = rng.integers(0, W, (N, 8, I, 16), dtype=np.int32); t = rng.integers(0, 256, (N, 8, I, 16), dtype=np.int32)
    a = rng.integers(0, 256, (N, 8, I), dtype=np.int32); c = rng.integers(0, W, (N, 8, 16, C), dtype=np.int32)
    w = rng.integers(0, 256, (N, 8, 16, 1), dtype=np.int32); th = rng.integers(60, 421, (N, 8, I), dtype=np.int32)
    s = rng.integers(0, 136, (N, 8, 16, I), dtype=np.int32)
    closed = rng.random((N, 8, I)) < 0.4
    b = np.where(closed, (a + np.add.reduce(t, axis=3)) & 255, rng.integers(0, 256, (N, 8, I))).astype(np.int32)
    f = look(x, s, s, l, t, a, b, np.zeros(N, np.int32))[0]
    noise = np.rint(rng.standard_normal((N, 8, 16, I)) * rng.choice(np.array([0, 4, 12, 30]), (N, 8, 1, I)))
    e = np.clip(s + np.where(closed[:, :, None, :], np.add.reduce(f, axis=4), 120) + noise, 0, 255).astype(np.int32)
    hit = (rng.random((N, 8, I, 1)) < 0.6) & (np.arange(16) == rng.integers(0, 16, (N, 8, I, 1)))
    t = np.where(hit, (t + rng.integers(1, 256, (N, 8, I, 1))) & 255, t).astype(np.int32)
    return x, s, e, l, t, a, b, c, w, th
def pack(x, s, e, l, t, a, b, c, w, th):
    return {"xt": np.asarray(x, np.float32).reshape(N, 128, W).astype(BF), "sp": np.asarray(s, np.float32).reshape(N, 128, I).astype(BF), "ep": np.asarray(e, np.float32).reshape(N, 128, I).astype(BF),
            "lg": unlegs(np.asarray(l, np.int32)), "tn": unlegs(np.asarray(t, np.int32)), "aa": np.asarray(a, np.int32), "bb": np.asarray(b, np.int32),
            "ct": np.ascontiguousarray(np.asarray(c, np.int32).reshape(N, 128, C)), "wt": np.ascontiguousarray(np.asarray(w, np.int32).reshape(N, 128, 1)), "th": np.asarray(th, np.int32)}
def setup_inputs(rng):
    return pack(*parts(rng))
def setup_inputs_spread(rng):
    x = np.minimum(16 * rng.random((N, 8, 1, W)) ** 0.5 * rng.random((N, 8, 16, W)) ** 0.7, 15).astype(np.int32)
    s = np.minimum(256 * rng.random((N, 8, 1, I)) * rng.random((N, 8, 16, I)) ** 0.5, 255).astype(np.int32)
    e = np.minimum(256 * rng.random((N, 8, 1, I)) ** 0.3 * rng.random((N, 8, 16, I)) ** 0.5, 255).astype(np.int32)
    l = np.minimum(W * rng.random((N, 8, I, 16)) ** rng.choice(np.array([0.25, 1.0, 3.0]), (N, 8, 1, 1)), W - 1).astype(np.int32)
    t = np.minimum(256 * rng.random((N, 8, I, 1)) * rng.random((N, 8, I, 16)), 255).astype(np.int32)
    a = np.minimum(256 * rng.random((N, 8, I)) ** 2, 255).astype(np.int32); b = rng.integers(0, 256, (N, 8, I))
    c = np.minimum(W * rng.random((N, 8, 16, C)) ** rng.choice(np.array([0.25, 1.0, 3.0]), (N, 8, 1, C)), W - 1).astype(np.int32)
    w = np.exp2(8 * rng.random((N, 8, 16, 1))).astype(np.int32) - 1; th = np.minimum(np.exp2(4 + 8 * rng.random((N, 8, I))).astype(np.int32) - 1, 4080)
    return pack(x, s, e, l, t, a, b, c, w, th)
def setup_inputs_ends(rng):
    share = rng.choice(np.array([0.03, 0.3, 0.5, 0.7, 0.97]), (N, 8, 1, 1)); share[0, 0] = 0.0; share[N - 1, 7] = 1.0
    x = 15 * (np.where(rng.random((N, 8, 1, W)) < 0.3, rng.random((N, 8, 16, W)), rng.random((N, 8, 1, W))) < share)
    alike = rng.random((N, 8, 1, I)) < 0.5
    s = 255 * np.where(alike, rng.integers(0, 2, (N, 8, 1, I)), rng.integers(0, 2, (N, 8, 16, I)))
    e = 255 * np.where(alike, rng.integers(0, 2, (N, 8, 1, I)), rng.integers(0, 2, (N, 8, 16, I)))
    for i, lo, hi in ((0, 255, 0), (1, 0, 255), (2, 0, 0), (I - 3, 0, 0), (I - 2, 0, 255), (I - 1, 255, 0)): s[..., i] = lo; e[..., i] = hi
    l = (W - 1) * rng.integers(0, 2, (N, 8, I, 16)); t = 255 * rng.integers(0, 2, (N, 8, I, 16)); l[:, :, I - 1] = W - 1; t[:, :, I - 1] = 255; l[:, :, 0] = 0; t[:, :, 0] = 0
    a = 255 * rng.integers(0, 2, (N, 8, I)); b = 255 * rng.integers(0, 2, (N, 8, I)); c = (W - 1) * rng.integers(0, 2, (N, 8, 16, C))
    w = 255 * rng.integers(0, 2, (N, 8, 16, 1)); w[:, 7] = 255; w[:, 3] = 0
    th = 4080 * rng.integers(0, 2, (N, 8, I)); th[:, ::2, I - 1] = 4080; th[:, 1::2, I - 1] = 0; th[:, 7, I - 1] = 4080 * (np.arange(N) & 1); th[:, 7, 0] = 4080 - th[:, 7, I - 1]
    return pack(x, s, e, l, t, a, b, c, w, th)
def setup_inputs_corners(rng):
    x, s, e, l, t, a, b, c, w, th = parts(rng)
    x[:, 1] = 7; e[:, 1, :, ::2] = np.minimum(s[:, 1, :, ::2] + 112, 255)
    x[:, 3] = 15 * (rng.random((N, 1, W)) < 0.5)
    l[:, 2] = rng.choice(np.array([0, W - 1, W // 2]), (N, I, 16)); c[:, 2] = rng.choice(np.array([0, W - 1, 1]), (N, 16, C)); l[:, 4] = rng.choice(np.array([0, W - 1, 5]), (N, I, 1))
    w[:, 5] = 0; w[:, 6] = 255; w[:, 0] = 255 * rng.integers(0, 2, (N, 16, 1))
    t[:, :, ::8, 0] = (t[:, :, ::8, 0] + 1) & 255; t[:, :, 4::8, 15] = (t[:, :, 4::8, 15] + 255) & 255
    m = np.min(look(x, s, e, l, t, a, b, np.zeros(N, np.int32))[4], axis=3)
    th = np.clip(m + rng.integers(-1, 2, m.shape), 0, 4080)
    return pack(x, s, e, l, t, a, b, c, w, th)
def setup_inputs_crowd(rng):
    x, s, e, l, t, a, b, c, w, th = parts(rng)
    w[:, 0] = 0; w[:, 1] = 255; s[:, 1] = 255
    w[:, 2] = 0; w[:, 2, 0] = 1; s[:, 2, 0] = 254 + rng.integers(0, 2, (N, I))
    w[:, 3] = 0; w[:, 3, 0] = 255; s[:, 3, 0] = 255
    for q in range(N): s[q, 3, 0, rng.integers(0, I)] = 1
    s[:, :, 0] = np.maximum(s[:, :, 0], 1); e[:, :, 0] = np.minimum(e[:, :, 0], s[:, :, 0] - 1)
    for q in range(N):
        g = int(rng.integers(0, 8)); i = int(rng.integers(0, I))
        if q < 4:
            th[q] = (0, 0, 4080, 4080)[q]
            if q & 1: th[q, g, i] = 4080 - th[q, g, i]
        else:
            th[q] = 4080 * rng.integers(0, 2, (8, 1)); th[q, g, i] = 4080 - th[q, g, i]; th[q, (g + 3) % 8, I - 1] = 4080 - th[q, (g + 3) % 8, I - 1]
    return pack(x, s, e, l, t, a, b, c, w, th)
def setup_inputs_falls(rng):
    x, s, e, l, t, a, b, c, w, th = parts(rng)
    e = np.minimum(np.maximum(e, s), s + 200)
    th[:] = 4079; x[:, 5, 0] = 0
    x[:, 6] = 15 - ((rng.integers(0, 16, (N, 1, W)) == np.arange(16)[:, None]) & (rng.random((N, 1, W)) < 0.03125)).astype(np.int32)
    z = rng.random((N, 1, I)) < 0.5; s[:, 6] = np.where(z, 0, s[:, 6]); e[:, 6] = np.where(z, 0, e[:, 6])
    q = int(rng.integers(0, N))
    for i in range(N):
        o = (q - ST * i) % N; n = 32 * int(rng.integers(0, I // 8)) + int(rng.integers(1, 32))
        n = (n, 0, n, 8 * I)[i & 3]
        m = (rng.permutation(8 * I) < n).reshape(8, 1, I)
        s[o] = np.where(m, 255, s[o]); e[o] = np.where(m, 0, e[o])
        near = ~m[5, 0] & (rng.random(I) < 0.25)
        s[o, 5] = np.where(near, 255, s[o, 5]); e[o, 5] = np.where(near, 0, e[o, 5]); s[o, 5, 0] = np.where(near, 254, s[o, 5, 0])
    return pack(x, s, e, l, t, a, b, c, w, th)
def check_inputs(d):
    bad = []
    for k, hi in (("xt", 15), ("sp", 255), ("ep", 255), ("lg", W - 1), ("tn", 255), ("aa", 255), ("bb", 255), ("ct", W - 1), ("wt", 255), ("th", 4080)):
        v = np.asarray(d[k]).astype(np.float64)
        if not (np.min(v) >= 0 and np.max(v) <= hi): bad.append("range of " + k)
        elif np.any(v != np.floor(v)): bad.append("whole numbers in " + k)
    return bad
def reference(xt, sp, ep, lg, tn, aa, bb, ct, wt, th):
    x = xt.astype(np.float32).astype(np.int32).reshape(N, 8, 16, W)
    s = sp.astype(np.float32).astype(np.int32).reshape(N, 8, 16, I); e = ep.astype(np.float32).astype(np.int32).reshape(N, 8, 16, I)
    l = legs(lg); t = legs(tn); a = aa.astype(np.int32); b = bb.astype(np.int32)
    c = ct.astype(np.int32).reshape(N, 8, 16, C); w = wt.astype(np.int32).reshape(N, 8, 16, 1)
    am = np.zeros(N, np.int32); leg = np.arange(16); slot = np.arange(I)
    for v in range(V):
        h = (np.arange(N) - ST * v) % N
        l0, t0, a0, b0 = l[h], t[h], a[h], b[h]
        f, g, p, tot, d = look(x, s[h], e[h], l0, t0, a0, b0, am)
        k = np.argmin(d, axis=3); ok = np.min(d, axis=3) <= th
        at = k[:, :, None, :, None]
        pk, fk, gk = [np.take_along_axis(z, at, 4)[..., 0] for z in (p, f, g)]
        u = np.add.reduce(w * np.minimum(pk, 255), axis=2)
        got = np.swapaxes(np.take_along_axis(c, (u % C)[:, :, None, :], 3), 2, 3)
        t[h] = np.where(ok[..., None] & (leg == k[..., None]), (t0 + (b0 + am[:, None, None] - a0)[..., None] - tot) & 255, t0)
        l[h] = np.where(~ok[..., None] & (leg >= k[..., None]), got, l0)
        pc = np.broadcast_to(((C // I) * slot + u % (C // I))[:, :, None, :], (N, 8, 16, I))
        np.put_along_axis(c, pc, np.where(ok[:, :, None, :], np.take_along_axis(c, pc, 3), np.swapaxes(l0, 2, 3)), 3)
        px = np.broadcast_to(((W // I) * slot + u % (W // I))[:, :, None, :], (N, 8, 16, I))
        np.put_along_axis(x, px, (fk + gk) >> 1, 3)
        am = (np.add.reduce((~ok).astype(np.int32), axis=(1, 2)) & 31).astype(np.int32)
    return {"yx": x.reshape(N, 128, W).astype(np.float32).astype(BF), "yl": unlegs(l).astype(np.float32), "yt": unlegs(t).astype(np.float32), "yc": c.reshape(N, 128, C).astype(np.float32)}

@@ -1,0 +1,599 @@
+from concourse.mybir import AluOpType as ALU, ActivationFunctionType as ACT
+
+N, V = 8, 5
+ROT = 167
+OVER = ROT % 16
+NOFF = 148.0 + 2.0 ** -10
+BIG, HOLD = 2.0 ** 24, 2.0 ** 22
+bf, f32, i32, u16 = "bfloat16", "float32", "int32", "uint16"
+
+SCRATCH = {}
+for _n, _c, _d in [
+        ("X", 2064, bf), ("C", 1024, f32), ("CI", 512, i32), ("CO", 512, f32), ("LI", 128, i32), ("TI", 128, i32), ("ABI", 128, i32),
+        ("EP", 128, bf), ("WI", 128, i32), ("WR", 128, bf), ("WM", 128, bf), ("THI", 128, i32), ("THF", 128, f32), ("THS", 128, f32),
+        ("THK", 8, f32), ("ONE", 128, bf), ("Q4", 128, bf), ("B4", 128, bf), ("TA", 128, bf), ("TB", 128, bf), ("T3A", 128, bf),
+        ("T3B", 128, bf), ("ID", 128, bf), ("NID", 128, bf), ("N64", 128, bf), ("B1", 128, bf), ("B16", 128, bf), ("SA", 128, bf),
+        ("SBB", 128, bf), ("SD", 128, bf), ("S8", 128, f32), ("PERM", 128, bf), ("E", 2048, bf), ("REP", 128, bf), ("DG", 144, bf),
+        ("HM", 128, bf), ("HM1", 128, bf), ("HM2", 128, bf), ("SELP", 144, bf), ("SELN", 144, bf), ("PI", 8, i32), ("PJ", 8, i32),
+        ("COL", 16, f32), ("IO", 16, i32), ("PL", 8, u16), ("BL", 8, u16), ("MK", 512, bf), ("RB", 64, bf), ("CR", 704, bf),
+        ("B0", 8, f32), ("BX", 16, f32), ("M128", 128, bf), ("R32", 128, f32),
+        ("F", 2064, bf), ("B", 2048, bf), ("PF", 2048, bf), ("SB", 2048, bf), ("AZ", 2048, bf), ("MZ", 2048, bf),
+        ("QQ", 384, bf), ("VI", 256, i32), ("VM", 256, i32), ("OFF", 256, u16), ("KEY", 128, i32), ("SP", 128, bf), ("KK", 16, i32),
+        ("LK", 8, u16), ("PR", 128, bf), ("PM", 128, bf), ("XX", 256, bf), ("HS", 128, i32), ("NWM", 128, bf), ("U5", 8, i32),
+        ("LU", 8, u16), ("U2", 16, i32), ("U3", 16, i32), ("U4", 16, i32), ("LS", 16, u16), ("OK5", 8, f32), ("M1", 128, f32),
+        ("G1", 128, bf), ("G2", 128, bf), ("GL", 128, f32), ("W255", 64, bf), ("FK", 128, bf), ("FB", 128, bf), ("AV", 128, bf),
+        ("NC", 8, f32), ("CJ", 128, f32), ("QA", 128, bf), ("AR", 128, bf), ("LR", 128, f32),
+        ("FL", 128, f32), ("FT", 128, f32), ("OL", 128, f32), ("OT", 128, f32)]:
+    SCRATCH[_n] = ("sbuf", [128, _c], _d)
+for _t in range(V):
+    SCRATCH["NL%d" % _t] = ("sbuf", [128, 128], f32)
+    SCRATCH["TT%d" % _t] = ("sbuf", [128, 128], bf)
+    SCRATCH["ST%d" % _t] = ("sbuf", [128, 384], bf)
+for _t in range(V - 1):
+    SCRATCH["NO%d" % _t] = ("sbuf", [128, 128], f32)
+    SCRATCH["TO%d" % _t] = ("sbuf", [128, 128], bf)
+for _n in ("Z0", "Z1", "I1", "J0", "J1", "P0", "P1", "CN"):
+    SCRATCH[_n] = ("psum", [128, 512], f32)
+
+CFG = {"chunks": [(0, 0, 8, "S", "V", "V"), (0, 8, 16, "S", "S", "V"), (1, 0, 7, "S", "V", "V"), (1, 7, 13, "S", "S", "V"), (1, 13, 16, "V", "S", "V")],
+       "ec": "S" * 9 + "V" * 7, "split": (1, 0), "bitu": False, "ttu": True, "xsplit": 1, "slack": 30, "bias": {},
+       "cv": 1.04, "g": 1.56, "sc": 3.8, "pe": 0.55, "lat": 90.0, "riss": 600.0, "rlat": 2600.0, "dlat": 2200.0}
+
+
+def A(name, lo=0, hi=None, step=1, p=128, p0=0):
+    return ("A", name, lo, SCRATCH[name][1][1] if hi is None else hi, step, p0, p)
+
+
+def IND(win, off):
+    return ("I", win, off)
+
+
+def D(name, lo=None, hi=None):
+    return ("D", name, lo, hi)
+
+
+def size(a):
+    return (a[3] - a[2] + abs(a[4]) - 1) // abs(a[4])
+
+
+def resolve(T, a):
+    if not isinstance(a, tuple):
+        return a
+    if a[0] == "I":
+        return resolve(T, a[1]).indirect(resolve(T, a[2]))
+    if a[0] == "D":
+        return T[a[1]][:] if a[2] is None else T[a[1]][:, a[2]:a[3]]
+    _, name, lo, hi, step, p0, p = a
+    if step == 1:
+        return T[name][p0:p, lo:hi]
+    if step == -1:
+        return T[name][p0:p, hi - 1::-1] if lo == 0 else T[name][p0:p, hi - 1:lo - 1:-1]
+    return T[name][p0:p, lo:hi:step]
+
+
+def place(o, eng):
+    o["eng"] = eng
+    o["call"], o["args"], o["kw"], o["dur"] = o["alt"][eng]
+
+
+def build_ops(cfg):
+    ops, acc, bank, now = [], {}, {}, [-1]
+    cv = cfg["cv"]
+
+    def add(eng, call, args, outs, ins, dur, kind="c", sem=None, lat=0.0, tag=None, after=(), kw=None, dst=0):
+        i = len(ops)
+        deps, order = set(), set(after)
+        items = []
+        for a, wr in [(x, True) for x in outs] + [(x, False) for x in ins]:
+            if not isinstance(a, tuple) or a[0] == "D":
+                continue
+            if a[0] == "I":
+                items += [(a[1], wr), (a[2], False)]
+            else:
+                items.append((a, wr))
+        for a, wr in items:
+            name, lo, hi = a[1], a[2], a[3]
+            if SCRATCH[name][0] == "psum":
+                st = bank.setdefault(name, [None, [], []])
+                if st[0] != eng:
+                    st[0], st[2], st[1] = eng, st[1], []
+                deps.update(st[2])
+                if eng == "P":
+                    order.update(st[1])
+                st[1].append(i)
+                continue
+            for (l2, h2, j, w2, t2) in acc.setdefault(name, []):
+                if l2 < hi and lo < h2 and (wr or w2) and not (tag is not None and t2 == tag):
+                    deps.add(j)
+        for a, wr in items:
+            name, lo, hi = a[1], a[2], a[3]
+            if SCRATCH[name][0] == "psum":
+                continue
+            if wr and abs(a[4]) == 1 and a[5] == 0 and a[6] == 128:
+                acc[name] = [e for e in acc[name] if not (lo <= e[0] and e[1] <= hi)]
+            acc[name].append((lo, hi, i, wr, tag if wr else None))
+        deps.discard(i)
+        order.discard(i)
+        ops.append({"eng": eng, "call": call, "args": args, "kw": kw or {}, "deps": deps, "order": order - deps, "dur": dur,
+                    "kind": kind, "sem": sem, "lat": lat, "dst": dst, "t": now[0]})
+        return i
+
+    def two(*aps):
+        return all(SCRATCH[a[1]][2] in (bf, u16) and SCRATCH[a[1]][0] == "sbuf" for a in aps)
+
+    def cost(o, ins, f):
+        if o[0] == "I":
+            return 55.0 + size(ins[0]) * cfg["sc"] * cv
+        if ins[0][0] == "I":
+            return 55.0 + size(o) * cfg["g"] * cv
+        return max(64.0, size(o) * f) * cv
+
+    def ts(o, i, s1, a, s2=None, b=None, tag=None):
+        args = [o, i, s1, s2, a] + ([] if b is None else [b])
+        return add("V", "tensor_scalar", args, [o], [i, s1, s2], cost(o, [i], 0.5 if i[0] == "A" and two(o, i) else 1.0), tag=tag)
+
+    def cp(o, i, tag=None):
+        return add("V", "tensor_copy", [o, i], [o], [i], cost(o, [i], 0.5 if i[0] == "A" and o[0] == "A" and two(o, i) else 1.0), tag=tag)
+
+    def tt(o, a, b, op):
+        ps = any(x[0] == "A" and SCRATCH[x[1]][0] == "psum" for x in (a, b))
+        return add("V", "tensor_tensor", [o, a, b, op], [o], [a, b], cost(o, [a], 1.0 if ps else 2.0))
+
+    def scan(o, d0, d1, op0, op1):
+        return add("V", "tensor_tensor_scan", [o, d0, d1, 0.0, op0, op1], [o], [d0, d1], cost(o, [d0], 0.5 if two(o, d0, d1) else 1.0))
+
+    def ms(o, c, tag=None):
+        return add("V", "memset", [o, c], [o], [], cost(o, [o], 0.5 if two(o) else 1.0), tag=tag)
+
+    def act(o, i, func, bias=0.0, scale=1.0, accum=None, tag=None):
+        kw = {"bias": bias, "scale": scale}
+        if accum is not None:
+            kw["accum_out"] = accum
+        return add("S", "activation", [o, i, func], [o] + ([accum] if accum else []), [i, bias, scale], 20.0 + cost(o, [i], 1.0), kw=kw, tag=tag)
+
+    def mm(lst):
+        dur = 30.0 + sum(max(min(64, size(m[1])), size(m[2])) * (4 if SCRATCH[m[2][1]][2] == f32 else 1) for m in lst) * cfg["pe"]
+        return add("P", "mm", lst, [m[0] for m in lst], [m[1] for m in lst] + [m[2] for m in lst], dur)
+
+    def aff(o, i, pat, op, base, cm):
+        return add("G", "affine_select", [o, i, pat, op, 0.0, base, cm], [o], [i], 190.0 + 2 * size(o) * cv)
+
+    def iota(o, pat, base, cm):
+        kw = {} if SCRATCH[o[1]][2] == i32 else {"allow_small_or_imprecise_dtypes": True}
+        return add("G", "iota", [o, pat, base, cm], [o], [], 150.0 + 2 * size(o) * cv, kw=kw)
+
+    def dma(eng, o, i, extra=0.0, tag=None):
+        return add(eng, "dma_start", [o, i], [o], [i], 120.0, kind="d", sem="d%d" % len(ops), lat=cfg["dlat"] + extra, tag=tag)
+
+    def send(o, i, dst, extra=0.0, after=()):
+        return add("G", "remote", [o, i], [o], [i], cfg["riss"], kind="r", sem="r%d" % len(ops), lat=cfg["rlat"] + extra, dst=dst, after=after)
+
+    def either(eng, o, i, tag=None):
+        k = cp(o, i, tag)
+        ops[k]["alt"] = {"V": ("tensor_copy", [o, i], {}, ops[k]["dur"]),
+                         "S": ("activation", [o, i, ACT.Identity], {"bias": 0.0, "scale": 1.0}, 20.0 + cost(o, [i], 1.0))}
+        place(ops[k], eng)
+        return k
+
+    def gather(eng, o, win, off):
+        return either(eng, o, IND(win, off))
+
+    def col(k):
+        return A("COL", k, k + 1)
+
+    add_, sub, mul, mn = ALU.add, ALU.subtract, ALU.mult, ALU.min
+    band, shr = ALU.bitwise_and, ALU.logical_shift_right
+
+    dma("S", A("TI"), D("tn"))
+    dma("S", A("ABI", p=8), D("aa"), tag="ab")
+    dma("S", A("ABI", p0=8, p=16), D("bb"), tag="ab")
+    dma("S", A("LI"), D("lg"))
+    dma("Y", A("X", ROT, 2048), D("xt", 0, 2048 - ROT), 1200.0)
+    dma("Y", A("X", 0, ROT), D("xt", 2048 - ROT, 2048), 1200.0)
+    dma("Y", A("SP"), D("sp"), 1200.0)
+    dma("Y", A("EP"), D("ep"), 1200.0)
+    dma("Y", A("WI", p=1), D("wt"), 1200.0)
+    dma("Y", A("THI", p=8), D("th"), 1200.0)
+    dma("Y", A("CI"), D("ct"), 1800.0)
+    ms(A("ONE"), 1.0); ms(A("Q4"), 0.25); ms(A("ST0", 256, 384), 0.0)
+    for lo, hi, c in ((0, 192, 1088.0), (192, 384, 9280.0), (384, 512, 1.125), (512, 576, 0.0)):
+        ms(A("CR", lo, hi, p=1), c)
+    iota(A("G1", p=16), [[-1, 8], [0, 16]], 0, 1)
+    iota(A("G2"), [[1, 128]], 0, -1)
+    iota(A("PI", 0, 1), [[1, 1]], 0, 1)
+    iota(A("IO", 0, 8), [[64, 2], [4, 4]], 0, 0)
+    aff(A("PERM"), A("ONE"), [[64, 2], [1, 16], [16, 4]], ALU.is_equal, 0, -1)
+    aff(A("REP", p=16), A("ONE", p=16), [[0, 8], [-1, 16]], ALU.is_equal, 0, 1)
+    iota(A("IO", 8, 16), [[1, 8]], 0, 0)
+    iota(A("CR", 576, 640, p=1), [[1, 64]], 0, 0)
+    iota(A("CR", 640, 704, p=1), [[-16, 4], [0, 16]], 0, 0)
+    eq = ALU.is_equal
+    ts(A("SA", p=16), A("G1", p=16), 0.0, eq, 0.25, mul); ts(A("SBB", p=16), A("G1", p=16), 8.0, eq, 0.25, mul)
+    tt(A("SD", p=16), A("SBB", p=16), A("SA", p=16), sub)
+    for z in ("Z0", "Z1"):
+        mm([(A(z, 0, 128), A("SA", p=8), A("SA", p=8), True, True)])
+    for name, op, c in (("TA", ALU.is_ge, 4.0), ("TB", ALU.is_lt, -4.0), ("T3A", ALU.not_equal, -4.0)):
+        ts(A(name), A("G2"), 0.0, op, c, mul)
+        tt(A(name), A("Z0", 0, 128), A(name), mul)
+    for name, c in (("T3B", -4.0), ("B4", 4.0), ("B1", 16.0), ("B16", 256.0)):
+        act(A(name), A("Z1", 0, 128), ACT.Identity, scale=c)
+    ts(A("N64"), A("G2"), 0.0, eq, -64.0, mul); ts(A("ID"), A("G2"), 0.0, eq); ts(A("NID"), A("G2"), 0.0, eq, -1.0, mul)
+    ks = 1024.0 if cfg["bitu"] else 64.0
+    ts(A("S8", p=8), A("G1", p=8), 0.0, eq, ks, mul)
+    if cfg["bitu"]:
+        iota(A("PR", p=1), [[0, 8], [64, 16]], 0, 0)
+    ts(A("PJ", 0, 1), A("PI", 0, 1), 15, band); ts(A("PJ", 1, 2), A("PI", 0, 1), 3, band); ts(A("PJ", 2, 3), A("PI", 0, 1), 2, shr, 3, band)
+    cp(col(0), A("PJ", 0, 1))
+    ts(col(8), A("PJ", 1, 2), 16.0, mul); tt(col(7), col(8), A("PJ", 2, 3), add_)
+    ts(A("PL"), A("IO", 0, 8), col(7), add_)
+    cp(A("BL"), A("IO", 8, 16))
+    ts(col(1), col(0), 16.0, add_);
+    if not cfg["bitu"]:
+        ts(col(2), col(0), 64.0, mul)
+    ts(col(4), col(0), 15.0, ALU.is_lt, HOLD, mul); ts(col(5), col(0), 4.0, mul); ts(col(6), col(0), 16.0, mul, float(ROT), add_)
+    ts(A("B0"), A("IO", 8, 16), 64.0, mul, col(5), add_)
+    ts(A("U3", 0, 8), A("IO", 8, 16), 256.0, mul, col(6), add_)
+    ts(A("U4", 0, 8), A("U3", 0, 8), 2047, band); cp(A("BX", 8, 16), A("U4", 0, 8))
+    cp(A("X", 2048, 2048 + OVER), A("X", 0, OVER)); ms(A("X", 2048 + OVER, 2064), 0.0)
+    ms(A("MK"), 1.0); ms(A("MK", 0, 512, 16), 0.0)
+    ms(A("RB"), 0.0); ms(A("RB", 0, 64, 16), BIG)
+    ms(A("F", 0, 16), 0.0); ms(A("DG", 0, 16), 0.0); ms(A("M128"), -136.0); ms(A("R32", p=1), 1.0 / 32)
+    ms(A("SELP"), 0.0); ts(A("SELP", 15, 143, 16), A("B4", 0, 128, 16), 4 * ks, mul)
+    if any(c[5] == "S" for c in cfg["chunks"]):
+        act(A("SELN"), A("SELP"), ACT.Identity, scale=-1.0)
+    for k in range(16):
+        either(cfg["ec"][k], A("E", k, 2048, 16), A("PERM"), tag="e")
+    mm([(A("P0", 0, 128), A("REP", p=16), A("REP", p=16), True, True)])
+    act(A("DG", 16, 144), A("P0", 0, 128), ACT.Identity)
+    act(A("HM1"), A("DG", 16, 144), ACT.Identity, scale=BIG); act(A("HM2"), A("DG", 15, 143), ACT.Identity, scale=-HOLD)
+    mm([(A("P0", 128, 256), A("ID"), A("HM1"), True, False), (A("P0", 128, 256), A("ID"), A("HM2"), False, True)])
+    act(A("HM"), A("P0", 128, 256), ACT.Identity)
+    cp(A("TT0"), A("TI")); cp(A("ST0", 256, 384, p=16), A("ABI", p=16)); ts(A("NL0"), A("LI"), NOFF, add_)
+    ts(A("ST0", 128, 256), A("SP"), -1.0, mul, 255.0, add_)
+    mm([(A("P1", 0, 128), A("SP"), A("ID"), True, False), (A("P1", 0, 128), A("EP"), A("NID"), False, True)])
+    act(A("ST0", 0, 128), A("P1", 0, 128), ACT.Identity)
+    last_send = send(A("ST1"), A("ST0"), 1, 1500.0)
+    cp(A("WR", p=1), A("WI", p=1))
+    mm([(A("CN", 0, 128), A("WR", p=1), A("ONE", p=1), True, True)])
+    tt(A("WM"), A("CN", 0, 128), A("B1"), mul)
+    act(A("NWM"), A("WM"), ACT.Identity, scale=-1.0); ms(A("W255"), 255.0)
+    cp(A("THF", p=8), A("THI", p=8))
+    mm([(A("CN", 128, 256), A("S8", p=8), A("THF", p=8), True, True)])
+    scan(A("THS"), A("HM"), A("CN", 128, 256), add_, mn)
+    ts(A("THK"), A("THS", 15, 128, 16), col(4), add_, ks - 1 - 4080 * ks, add_)
+    ts(A("C", 0, 512), A("CI"), NOFF, add_)
+
+    def index(t, h, b0, b1):
+        c0, c1, J, ST, TT = 64 * h, 64 * h + 64, "J%d" % h, "ST%d" % t, "TT%d" % t
+        one = A("ONE", p=1)
+        ab = A(ST, 256 + c0, 256 + c1, p=16)
+        tq = A(TT, c0, c1)
+        x0, x1 = 64 * b0, 64 * b1
+        qq = A("QQ", 192 * h + x0, 192 * h + x1)
+        with_a = t > 0 and b1 == 3
+        for bk in ("I1", J):
+            end = bk == "I1"
+            rows = (0,) if end else (192, 384)
+            mm([(A(bk, x0, x1), one, A("CR", r + x0, r + x1, p=1), r < 384, False) for r in rows])
+            mm([(A(bk, 64 * b, 64 * b + 64), A(("SA", "SBB", "SD")[b], p=16), ab, False, False) for b in range(b0, b1)])
+            w = ("TA", "TB", "T3A" if end else "T3B")
+            mm([(A(bk, 64 * b, 64 * b + 64), A(w[b]), tq, False, end and not with_a and b == b1 - 1) for b in range(b0, b1)])
+            if with_a:
+                mm([(A(bk, 64, 192), A("AR", p=1), A("Q4", p=1), False, end)])
+            if end:
+                act(qq, A("I1", x0, x1), ACT.Identity, bias=127.5 + 1.0 / 512, scale=1.0 / 64)
+        mm([(A(J, x0, x1), A("N64"), qq, False, True)])
+        v0, v1 = 128 * h + x0, 128 * h + min(x1, 128)
+        for b in range(b0, min(b1, 2)):
+            tt(A("VI", 128 * h + 64 * b, 128 * h + 64 * b + 64), A(J, 64 * b, 64 * b + 64), A("NL%d" % t, c0, c1), mul)
+        pl = A("PL", 0, (v1 - v0) // 16)
+        if cfg["bitu"]:
+            ts(A("OFF", v0, v1), IND(A("VI", v0, v1), pl), 2047, band)
+        else:
+            ts(A("VM", v0, v1), A("VI", v0, v1), 2047, band)
+            cp(A("OFF", v0, v1), IND(A("VM", v0, v1), pl))
+
+    def big(t, q):
+        h, p0, p1, gf, gb, ce = cfg["chunks"][q]
+        n0, n1, Z = 1024 * h + 64 * p0, 1024 * h + 64 * p1, A("Z%d" % (q % 2), 0, 64 * (p1 - p0))
+        o0, o1 = 128 * h + 4 * p0, 128 * h + 4 * p1
+        mk = A("MK", 0, n1 - n0)
+        gather(gf, A("F", 16 + n0, 16 + n1), A("X", 0, 2048), A("OFF", o0, o1))
+        gather(gb, A("B", n0, n1), A("X", 0, 2048), A("OFF", o0 + 64, o1 + 64))
+        scan(A("PF", n0, n1), A("F", 15 + n0, 15 + n1), mk, add_, mul)
+        scan(A("SB", n0, n1, -1), mk, A("B", n0, n1, -1), mul, add_)
+        mm([(Z, A("ST%d" % t, 0, 128), A("E", n0, n1), True, False)])
+        mm([(Z, A("ID"), A("PF", n0, n1), False, False)])
+        mm([(Z, A("ID"), A("SB", n0, n1), False, True)])
+        act(A("AZ", n0, n1), Z, ACT.Abs)
+        if ce == "V":
+            ts(A("MZ", n0, n1), A("AZ", n0, n1), 255.0, sub, 0.0, mn)
+        else:
+            act(A("MZ", n0, n1), A("AZ", n0, n1), ACT.Relu, bias=255.0, scale=-1.0)
+        sel = "SELP" if ce == "V" else "SELN"
+        dd = A("P%d" % h, 0, 64)
+        lst = [(dd, A("ONE", p=1), A("CR", 576, 640, p=1), True, False)] if p0 == 0 else []
+        if p0 == 0 and cfg["bitu"]:
+            lst.append((dd, A("PR", p=1), A("ONE", 0, 64, p=1), False, False))
+        for p in range(p0, p1):
+            lst.append((dd, A(sel, 15 - p, 143 - p), A("MZ", 1024 * h + 64 * p, 1024 * h + 64 * p + 64), False, p == 15))
+        mm(lst)
+
+    def post(t, h, prev):
+        c0, c1, l0, l1, P, J = 64 * h, 64 * h + 64, 4 * h, 4 * h + 4, "P%d" % h, "J%d" % h
+        last = t == V - 1
+        key = A("KEY", c0 + 15, c1, 16)
+        kk, ok = (A("KK", 0, 4), A("KK", 4, 8)) if h == 0 else (A("KK", 12, 16), A("KK", 8, 12))
+        xk, xo = (A("XX", 0, 64), A("XX", 64, 128)) if h == 0 else (A("XX", 192, 256), A("XX", 128, 192))
+        scan(A("KEY", c0, c1), A("RB"), A(P, 0, 64), add_, mn)
+        ts(kk, key, 63, band)
+        if cfg["bitu"]:
+            ts(A("LK", l0, l1), key, 1023, band)
+        else:
+            ts(A("LK", l0, l1), kk, col(2), add_)
+        tt(ok, key, A("THK", l0, l1), ALU.is_le)
+        pf, room = IND(A("PF", 1024 * h, 1024 * h + 1024), A("LK", l0, l1)), A("ST%d" % t, 128 + c0, 128 + c1)
+        tt(A("PM", c0, c1), pf, room, mn)
+        mm([(A(P, 128, 192), A("WM"), A("W255"), True, False), (A(P, 128, 192), A("NWM"), room, False, False)])
+        mm([(A(P, 128, 192), A("WM"), A("PM", c0, c1), False, True)])
+        tt(A("XX", 128 * h, 128 * h + 128), IND(A("KK", 8 * h, 8 * h + 8), A("BL")), A("DG", 16, 144), mul)
+        bc = A("CN", c0, c1)
+        mm([(bc, A("ONE", p=1), A("CR", 640, 704, p=1), True, False), (bc, A("B1"), xk, False, False), (bc, A("B16"), xo, False, True)])
+        if not last:
+            mm([(A("P0", 256 + c0, 256 + c1, p=1), A("ONE", 0, 1), xo, True, True)])
+            if h == 1:
+                nc = A("NC", 0, 1, p=1)
+                act(A("CJ", p=1), A("P0", 256, 384, p=1), ACT.Identity, bias=42.0, scale=-1.0, accum=nc)
+                act(A("QA", p=1), A("R32", p=1), ACT.Identity, bias=-0.484375, scale=nc)
+                act(A("AR", p=1), A("QA", p=1), ACT.Identity, bias=nc, scale=-32.0)
+        scan(A("HS", c0, c1), A("HM", 0, 64), A(P, 128, 192), add_, mn)
+        if cfg["bitu"]:
+            ts(A("LU", l0, l1), A("HS", c0 + 15, c1, 16), 511, band)
+        else:
+            ts(A("U5", l0, l1), A("HS", c0 + 15, c1, 16), 511, band)
+            cp(A("LU", l0, l1), A("U5", l0, l1))
+        m2, dt, gm = A(J, 192, 256), A(J, 256, 320), A(J, 320, 384)
+        ts(A("M1", c0, c1), bc, col(1), ALU.is_equal, 4.0, mul)
+        w_m2 = ts(m2, bc, col(0), ALU.is_le)
+        w_dt = tt(dt, A(J, 128, 192), A("M1", c0, c1), mul)
+        to, no = (A("OT", c0, c1), A("OL", c0, c1)) if last else (A("TO%d" % t, c0, c1), A("NO%d" % t, c0, c1))
+        ops[tt(to, dt, A("TT%d" % t, c0, c1), add_)]["deps"].add(w_dt)
+        dst = N - (V - 1) if last else 1
+        s1 = send(A("FT" if last else "TT%d" % (t + 1), c0, c1), to, dst, after=[prev])
+        nl = A("NL%d" % t, c0, c1)
+        if last:
+            act(A("LR", c0, c1), nl, ACT.Identity, bias=-NOFF)
+        tt(A("GL", c0, c1), IND(A("C", 0, 512), A("LU", l0, l1)), nl, sub)
+        w_gm = tt(gm, m2, A("GL", c0, c1), mul)
+        ops[w_gm]["deps"].add(w_m2)
+        ops[tt(no, gm, A("LR", c0, c1) if last else nl, add_)]["deps"].add(w_gm)
+        s2 = send(A("FL" if last else "NL%d" % (t + 1), c0, c1), no, dst, after=[s1])
+        if last:
+            dma("Y", D("yt", c0, c1), A("FT", c0, c1))
+            dma("Y", D("yl", c0, c1), A("FL", c0, c1))
+        return s2
+
+    def records(h0, h1):
+        c0, c1, l0, l1 = 64 * h0, 64 * h1, 8 + 4 * h0, 8 + 4 * h1
+        for h in range(h0, h1):
+            n0, lk, av = 1024 * h, A("LK", 4 * h, 4 * h + 4), A("P%d" % h, 192, 256)
+            fk, bk = A("FK", 64 * h, 64 * h + 64), A("FB", 64 * h, 64 * h + 64)
+            gather("S", fk, A("F", 16 + n0, 1040 + n0), lk)
+            gather("S", bk, A("B", n0, n0 + 1024), lk)
+            mm([(av, A("ID"), fk, True, False), (av, A("ID"), bk, False, True)])
+            act(A("AV", 64 * h, 64 * h + 64), av, ACT.Identity, bias=135.75, scale=0.5)
+        ts(A("U2", l0, l1), A("HS", c0 + 15, c1, 16), 15, band)
+        tt(A("LS", l0, l1), A("U2", l0, l1), A("BX", l0, l1), add_)
+        tt(IND(A("X"), A("LS", l0, l1)), A("AV", c0, c1), A("M128", c0, c1), add_)
+        if h1 == 2:
+            cp(A("X", 0, OVER), A("X", 2048, 2048 + OVER))
+
+    def controls(t):
+        ts(A("OK5"), A("KK", 4, 12), 512.0, mul)
+        tt(A("BX", 0, 8), A("OK5"), A("B0"), add_)
+        ts(A("U2", 0, 8), A("HS", 15, 128, 16), 3, band)
+        tt(A("LS", 0, 8), A("U2", 0, 8), A("BX", 0, 8), add_)
+        cp(IND(A("C"), A("LS", 0, 8)), A("NL%d" % t))
+
+    for t in range(V):
+        now[0] = t
+        for h in range(2):
+            if cfg["split"][h] and t > 0:
+                index(t, h, 0, 1); index(t, h, 1, 3)
+            else:
+                index(t, h, 0, 3)
+        for q in range(len(cfg["chunks"])):
+            big(t, q)
+        last_send = post(t, 0, last_send)
+        if cfg["xsplit"]:
+            records(0, 1)
+        last_send = post(t, 1, last_send)
+        if t + 2 < V:
+            last_send = send(A("ST%d" % (t + 2)), A("ST0"), t + 2, 1500.0, after=[last_send])
+        records(1 if cfg["xsplit"] else 0, 2)
+        controls(t)
+    dma("Y", D("yx", 0, 2048 - ROT), A("X", ROT, 2048), 1200.0)
+    dma("S", D("yx", 2048 - ROT, 2048), A("X", 0, ROT))
+    act(A("CO"), A("C", 0, 512), ACT.Identity, bias=-NOFF)
+    dma("S", D("yc"), A("CO"), 600.0)
+    return ops
+
+
+def label(o):
+    a, b = (o["args"][-1][0], o["args"][-1][2]) if o["call"] == "mm" else (o["args"][0], o["args"][0])
+    a = a[2] if a[0] == "I" else a
+
+    def short(x):
+        return (x[1][:2] if x[1][:2] in ("NL", "TT", "ST", "NO", "TO") else x[1]) + "_" + str(x[2])
+    return o["eng"] + short(a) + (short(b) if o["call"] == "mm" else "s" if b[0] == "I" else "")
+
+
+def schedule(ops, cfg):
+    n = len(ops)
+    succ = [[] for _ in ops]
+    for i, o in enumerate(ops):
+        for j in o["deps"] | o["order"]:
+            succ[j].append(i)
+    lat = cfg["lat"]
+    prio = [0.0] * n
+    for i in range(n - 1, -1, -1):
+        o = ops[i]
+        prio[i] = o["dur"] + o["lat"] + max([prio[k] + lat for k in succ[i]] + [0.0])
+    bias = cfg.get("bias", {})
+    prio = [x + bias.get(label(o), 0.0) for x, o in zip(prio, ops)]
+    left = [len(o["deps"] | o["order"]) for o in ops]
+    ready = {e: [] for e in "VSPGY"}
+    at = [0.0] * n
+    for i, o in enumerate(ops):
+        if left[i] == 0:
+            ready[o["eng"]].append(i)
+    free = {e: 0.0 for e in "VSPGY"}
+    queue = {e: [] for e in "VSPGY"}
+    start, done = [0.0] * n, [0.0] * n
+    slack = cfg.get("slack", 60.0)
+    for _ in range(n):
+        e = min((x for x in "VSPGY" if ready[x]), key=lambda x: max(free[x], min(at[i] for i in ready[x])))
+        t0 = max(free[e], min(at[i] for i in ready[e]))
+        i = max((k for k in ready[e] if at[k] <= t0 + slack), key=lambda k: (prio[k], -k))
+        ready[e].remove(i)
+        o = ops[i]
+        start[i] = max(free[e], at[i])
+        free[e] = start[i] + o["dur"]
+        done[i] = free[e] + o["lat"]
+        queue[e].append(i)
+        for k in succ[i]:
+            at[k] = max(at[k], done[i] + lat if i in ops[k]["deps"] else start[i])
+            left[k] -= 1
+            if left[k] == 0:
+                ready[ops[k]["eng"]].append(k)
+    return queue, start, done
+
+
+def timed(ops, queue, cfg):
+    start, done = [None] * len(ops), [None] * len(ops)
+    at, free, left = {e: 0 for e in queue}, {e: 0.0 for e in queue}, len(ops)
+    while left:
+        before = left
+        for e, q in queue.items():
+            while at[e] < len(q) and all(done[j] is not None for j in ops[q[at[e]]]["deps"]):
+                i = q[at[e]]
+                start[i] = max([free[e]] + [done[j] + cfg["lat"] for j in ops[i]["deps"]])
+                free[e] = start[i] + ops[i]["dur"]
+                done[i] = free[e] + ops[i]["lat"]
+                at[e] += 1
+                left -= 1
+        assert left < before
+    return start, done
+
+
+def plan_waits(ops, queue, start):
+    mark = {}
+    for e, q in queue.items():
+        c = 0
+        for i in q:
+            o = ops[i]
+            if o["kind"] == "c":
+                c += 1
+                mark[i] = ("e" + e, c)
+            else:
+                mark[i] = (o["sem"], 1)
+    know = {e: {} for e in queue}
+    seen, waits = {}, {}
+    pos = {i: k for q in queue.values() for k, i in enumerate(q)}
+    for i in sorted(range(len(ops)), key=lambda k: (start[k], pos[k])):
+        o = ops[i]
+        kn = know[o["eng"]]
+        w = {}
+        for j in sorted(o["deps"], key=lambda k: -start[k]):
+            s, c = mark[j]
+            if kn.get(s, 0) >= c:
+                continue
+            w[s] = max(w.get(s, 0), c)
+            kn[s] = c
+            if ops[j]["kind"] != "r":
+                for s2, c2 in seen[j].items():
+                    if kn.get(s2, 0) < c2:
+                        kn[s2] = c2
+        seen[i] = dict(kn)
+        waits[i] = w
+    total = {}
+    for s, c in mark.values():
+        total[s] = max(total.get(s, 0), c)
+    rest = [(s, c) for s, c in total.items() if not any(waits[i].get(s, 0) >= c for i in waits)]
+    return mark, waits, rest
+
+
+OPS = build_ops(CFG)
+ORDER = {
+    "V": "70 -59 54 -51 -1 60 -46 39 -50 12 -13 2 19 -4 2 3 -4 15 -5 4 -12 43 -28 -21 13 46 -5 15 -1 -23 -23 48 -53 -2 23 -15 -3 4 32 -29 13 54 -1 -38 40 -79 80 -25 4 5 30 -26 27 1 -87 1 80 -1 -28 30 14 -13 14 8 -51 -40 78 -35 45 4 1 -49 76 -17 18 2 -133 132 5 -3 -22 31 1 1 -5 6 -5 -18 19 -20 26 -40 41 -147 148 -32 38 -153 125 -122 -2 10 145 -154 8 147 2 -1 -4 9 -3 -5 17 -3 5 -4 16 -11 -4 2 4 10 -9 -227 45 183 9 15 -11 -194 192 -1 15 1 -14 25 -23 24 -23 24 17 -1 11 -9 10 -16 -1 2 1 9 10 3 29 -28 29 2 -1 5 -3 -31 40 -3 5 -4 5 -4 2 4 -36 37 -36 37 6 -34 1 -15 10 39 -29 30 1 1 2 -1 5 -3 30 -18 -3 5 -4 5 11 -15 2 18 -14 15 11 -25 9 17 -25 9 17 -16 27 -23 24 -23 24 17 -1 11 -9 10 -16 -1 2 1 9 13 -3 4 1 27 -17 18 2 -1 5 -3 -22 31 1 1 -5 6 -5 -19 20 -19 25 -40 41 7 -6 -32 39 -29 31 1 2 -1 5 -3 -5 17 -3 5 -4 5 -4 15 -13 4 15 -14 9 3 -11 9 15 -12 13 -15 4 12 -11 22 1 1 17 -1 11 -9 10 -16 -1 2 1 9 10 3 29 -28 29 2 -1 5 -3 -31 40 -3 5 -4 5 -4 2 4 -36 37 -36 37 -28 1 -15 48 -38 39 -29 30 1 1 2 -1 5 -3 29 1 -18 -3 5 11 -10 -5 3 29 -31 32 -26 27 -26 8 -7 8 1 27 -24 1 24 -23 24 17 -1 11 -9 10 -16 -1 2 1 9 13 -3 4 1 27 -17 18 2 -1 5 -3 -22 30 -3 -16 21 -4 -18 23 -4 2 -35 40 6 -5 -31 40 -30 31 1 1 -11 12 2 -1 5 -3 28 -20 -3 5 -4 5 -4 2 5 1 1 8 6 -1 2 -6 1 6 -5",
+    "S": "2 -1 -1 3 35 3 -2 1 49 -2 -6 9 -13 9 6 -17 1 41 -37 14 -12 11 -14 23 27 9 10 1 -53 49 13 -3 14 -62 61 10 1 -14 10 10 25 1 2 31 -1 -16 1 31 -30 17 25 23 10 1 -21 17 10 3 10 1 42 -32 -1 -13 45 -35 10 28 30 1 15 -32 1 18 -17 42 23 10 1 -21 17 10 3 11 -1 11 -1 -13 10 36 -26 25 3 30 1 -17 1 31 -13 -17 42 23 10 1 -21 17 10 3 10 11 -1 32 -41 -4 46 -36 10 28 30 -1 16 -31 1 17 -16 41 23 67 -57 1 -21 17 10 3 11 -1 11 -1 -13 48 -38 10 30 29 -1 -7 10 12 -1 2",
+    "P": "31 -1 100 -16 -23 27 -3 1 3 1 1 5 1 -26 27 3 -36 37 1 9 -37 38 1 8 -42 43 1 8 -15 10 15 -9 1 32 -3 1 3 -24 1 8 1 1 -17 10 10 25 44 1 51 -86 3 -2 3 72 -53 13 2 1 1 1 4 1 1 1 15 -13 1 1 1 1 4 6 13 -18 1 1 4 1 21 -9 -11 21 -7 10 5 94 1 -64 -21 24 -2 3 -34 1 9 1 8 1 1 28 -45 10 10 111 -76 86 -83 -2 3 32 -13 15 1 1 1 4 1 1 1 2 1 1 1 1 9 1 -6 19 -18 6 1 -6 1 26 -9 -11 21 8 -15 10 6 1 8 24 -3 1 3 -24 1 82 1 -75 1 1 -17 10 10 121 -96 86 -76 3 -2 3 19 15 1 1 -4 5 4 1 1 1 2 1 1 1 1 9 -5 1 18 -13 1 1 -6 1 26 -9 -11 21 -7 10 15 83 1 -63 -31 34 -2 3 -34 1 9 1 8 1 1 28 -45 10 10 120 -10 -75 3 -2 34 -31 33 1 1 1 -18 22 1 1 3 -2 3 1 1 1 4 1 4 14 -13 1 1 -6 1 26 -9 -11 21 8 -15 10 6 1 8 21 3 -2 -21 1 8 1 1 -17 47 -37 10 37 3 -2 20",
+    "G": "18 1 1 1 1 1 2 -1 2 77 102 4 28 4 1 119 4 28 4 1 119 4 28 4 1 119 4 28 4 118 5 26 5",
+    "Y": "4 1 1 1 1 1 1 823 1 45 -15 1",
+}
+if ORDER:
+    QUEUE = {}
+    for _e, _s in ORDER.items():
+        QUEUE[_e] = []
+        for _w in _s.split():
+            QUEUE[_e].append((QUEUE[_e][-1] if QUEUE[_e] else 0) + int(_w))
+        for _i in QUEUE[_e]:
+            if _i < len(OPS) and "alt" in OPS[_i] and _e in "VS":
+                place(OPS[_i], _e)
+    if sorted(i for q in QUEUE.values() for i in q) != list(range(len(OPS))) or any(OPS[i]["eng"] != e for e, q in QUEUE.items() for i in q):
+        QUEUE = schedule(OPS, CFG)[0]
+else:
+    QUEUE = schedule(OPS, CFG)[0]
+START, DONE = timed(OPS, QUEUE, CFG)
+MARK, WAITS, REST = plan_waits(OPS, QUEUE, START)
+KIND = {o["sem"]: o["kind"] for o in OPS if o["sem"]}
+SEMAPHORES = ["eV", "eS", "eP", "eG", "sent"] + list(KIND)
+
+
+def rank_program(g, core, T, topo):
+    rank = T.rank_of(core)
+    if rank is None:
+        return
+    engs = {"V": g.vector, "S": g.scalar, "P": g.tensor, "G": g, "Y": g.sync}
+    arrive = {}
+    for o in OPS:
+        if o["kind"] == "r":
+            arrive[o["sem"]] = len(topo.engines(T.cores[(rank - o["dst"]) % N], core))
+
+    def count(s, c):
+        return c if s not in KIND else 16 if KIND[s] == "d" else arrive[s]
+
+    sent = 0
+    for e, q in QUEUE.items():
+        eng = engs[e]
+        for i in q:
+            o = OPS[i]
+            for s, c in WAITS[i].items():
+                eng.wait_ge(T.sem[s], count(s, c))
+            call = o["call"]
+            if call == "remote":
+                d = T.cores[(rank + o["dst"]) % N]
+                rid, pid = topo.addr(d, core)
+                g.remote_dma(resolve(T, o["args"][0]), resolve(T, o["args"][1]), T.sem[o["sem"]], T.sem.sent, pid, rid, topo.mask(core, d))
+                sent += len(topo.engines(core, d))
+                continue
+            if call == "mm":
+                for m in o["args"]:
+                    ins = eng.matmul(resolve(T, m[0]), resolve(T, m[1]), resolve(T, m[2]), m[3], m[4])
+            else:
+                a = [resolve(T, x) for x in o["args"]]
+                kw = {k: resolve(T, x) for k, x in o["kw"].items()}
+                if call == "tensor_scalar": ins = eng.tensor_scalar(*a)
+                elif call == "tensor_copy": ins = eng.tensor_copy(*a)
+                elif call == "tensor_tensor": ins = eng.tensor_tensor(*a)
+                elif call == "tensor_tensor_scan": ins = eng.tensor_tensor_scan(*a)
+                elif call == "memset": ins = eng.memset(*a)
+                elif call == "activation": ins = eng.activation(*a, **kw)
+                elif call == "affine_select": ins = eng.affine_select(*a)
+                elif call == "iota": ins = eng.iota(*a, **kw)
+                else: ins = eng.dma_start(*a)
+            s = MARK[i][0]
+            ins.then_inc(T.sem[s], 16 if o["kind"] == "d" else 1)
+    g.wait_ge(T.sem.sent, sent)
+    for s, c in REST:
+        g.wait_ge(T.sem[s], count(s, c))

@@ -15,11 +15,11 @@ for _n, _c, _d in [
         ("T3B", 128, bf), ("ID", 128, bf), ("NID", 128, bf), ("N64", 128, bf), ("B1", 128, bf), ("B16", 128, bf), ("SA", 128, bf),
         ("SBB", 128, bf), ("SD", 128, bf), ("S8", 128, f32), ("PERM", 128, bf), ("E", 2048, bf), ("REP", 128, bf), ("DG", 144, bf),
         ("HM", 128, bf), ("HM1", 128, bf), ("HM2", 128, bf), ("SELP", 144, bf), ("SELN", 144, bf), ("PI", 8, i32), ("PJ", 8, i32),
-        ("COL", 16, f32), ("IO", 16, i32), ("PL", 8, u16), ("BL", 8, u16), ("MK", 512, bf), ("RB", 64, bf), ("CR", 704, bf),
+        ("COL", 16, f32), ("IO", 16, i32), ("PL", 8, u16), ("BL", 8, u16), ("MK", 512, bf), ("RB", 64, bf), ("LB", 8, f32),
         ("B0", 8, f32), ("BX", 16, f32), ("M128", 128, bf), ("R32", 128, f32),
         ("F", 2064, bf), ("B", 2048, bf), ("PF", 2048, bf), ("SB", 2048, bf), ("AZ", 2048, bf), ("MZ", 2048, bf),
         ("QQ", 384, bf), ("VI", 256, i32), ("VM", 256, i32), ("OFF", 256, u16), ("KEY", 128, i32), ("SP", 128, bf), ("KK", 16, i32),
-        ("LK", 8, u16), ("PR", 128, bf), ("PM", 128, bf), ("XX", 256, bf), ("HS", 128, i32), ("NWM", 128, bf), ("U5", 8, i32),
+        ("LK", 8, u16), ("SD2", 128, bf), ("PM", 128, bf), ("XX", 256, bf), ("HS", 128, i32), ("NWM", 128, bf), ("U5", 8, i32),
         ("LU", 8, u16), ("U2", 16, i32), ("U3", 16, i32), ("U4", 16, i32), ("LS", 16, u16), ("OK5", 8, f32), ("M1", 128, f32),
         ("G1", 128, bf), ("G2", 128, bf), ("GL", 128, f32), ("W255", 64, bf), ("FK", 128, bf), ("FB", 128, bf), ("AV", 128, bf),
         ("NC", 8, f32), ("CJ", 128, f32), ("QA", 128, bf), ("AR", 128, bf), ("LR", 128, f32),
@@ -114,6 +114,7 @@ def build_ops(cfg):
             acc[name].append((lo, hi, i, wr, tag if wr else None))
         deps.discard(i)
         order.discard(i)
+        dur += cfg.get("ov" + eng, 0.0)
         ops.append({"eng": eng, "call": call, "args": args, "kw": kw or {}, "deps": deps, "order": order - deps, "dur": dur,
                     "kind": kind, "sem": sem, "lat": lat, "dst": dst, "t": now[0]})
         return i
@@ -171,7 +172,7 @@ def build_ops(cfg):
     def either(eng, o, i, tag=None):
         k = cp(o, i, tag)
         ops[k]["alt"] = {"V": ("tensor_copy", [o, i], {}, ops[k]["dur"]),
-                         "S": ("activation", [o, i, ACT.Identity], {"bias": 0.0, "scale": 1.0}, 20.0 + cost(o, [i], 1.0))}
+                         "S": ("activation", [o, i, ACT.Identity], {"bias": 0.0, "scale": 1.0}, 20.0 + cfg.get("ovS", 0.0) + cost(o, [i], 1.0))}
         place(ops[k], eng)
         return k
 
@@ -195,21 +196,22 @@ def build_ops(cfg):
     dma("Y", A("WI", p=1), D("wt"), 1200.0)
     dma("Y", A("THI", p=8), D("th"), 1200.0)
     dma("Y", A("CI"), D("ct"), 1800.0)
-    ms(A("ONE"), 1.0); ms(A("Q4"), 0.25); ms(A("ST0", 256, 384), 0.0)
-    for lo, hi, c in ((0, 192, 1088.0), (192, 384, 9280.0), (384, 512, 1.125), (512, 576, 0.0)):
-        ms(A("CR", lo, hi, p=1), c)
-    iota(A("G1", p=16), [[-1, 8], [0, 16]], 0, 1)
-    iota(A("G2"), [[1, 128]], 0, -1)
+    ms(A("ONE"), 1.0); ms(A("Q4"), 0.25); ms(A("ST0", 256, 384), 1.0)
     iota(A("PI", 0, 1), [[1, 1]], 0, 1)
+    iota(A("G1", p=32), [[-1, 8], [0, 16]], 0, 1)
+    iota(A("G2"), [[1, 128]], 0, -1)
     iota(A("IO", 0, 8), [[64, 2], [4, 4]], 0, 0)
     aff(A("PERM"), A("ONE"), [[64, 2], [1, 16], [16, 4]], ALU.is_equal, 0, -1)
     aff(A("REP", p=16), A("ONE", p=16), [[0, 8], [-1, 16]], ALU.is_equal, 0, 1)
     iota(A("IO", 8, 16), [[1, 8]], 0, 0)
-    iota(A("CR", 576, 640, p=1), [[1, 64]], 0, 0)
-    iota(A("CR", 640, 704, p=1), [[-16, 4], [0, 16]], 0, 0)
     eq = ALU.is_equal
-    ts(A("SA", p=16), A("G1", p=16), 0.0, eq, 0.25, mul); ts(A("SBB", p=16), A("G1", p=16), 8.0, eq, 0.25, mul)
-    tt(A("SD", p=16), A("SBB", p=16), A("SA", p=16), sub)
+    ts(col(9), A("PI", 0, 1), 16.0, eq, 9280.0, mul); ts(col(10), A("PI", 0, 1), 17.0, eq, 1.125, mul); tt(col(9), col(9), col(10), add_)
+    c9 = A("COL", 9, 10, p=32)
+    ts(A("SA", p=32), A("G1", p=32), 0.0, eq, 0.25, mul); ts(A("SBB", p=32), A("G1", p=32), 8.0, eq, 0.25, mul)
+    ts(A("SBB", p=32), A("SBB", p=32), c9, add_)
+    tt(A("SD", p=32), A("SBB", p=32), A("SA", p=32), sub)
+    ts(A("SD2", p=32), A("SD", p=32), A("COL", 10, 11, p=32), sub)
+    ts(A("SA", p=32), A("SA", p=32), c9, add_)
     for z in ("Z0", "Z1"):
         mm([(A(z, 0, 128), A("SA", p=8), A("SA", p=8), True, True)])
     for name, op, c in (("TA", ALU.is_ge, 4.0), ("TB", ALU.is_lt, -4.0), ("T3A", ALU.not_equal, -4.0)):
@@ -218,25 +220,22 @@ def build_ops(cfg):
     for name, c in (("T3B", -4.0), ("B4", 4.0), ("B1", 16.0), ("B16", 256.0)):
         act(A(name), A("Z1", 0, 128), ACT.Identity, scale=c)
     ts(A("N64"), A("G2"), 0.0, eq, -64.0, mul); ts(A("ID"), A("G2"), 0.0, eq); ts(A("NID"), A("G2"), 0.0, eq, -1.0, mul)
-    ks = 1024.0 if cfg["bitu"] else 64.0
+    ks = 16.0
     ts(A("S8", p=8), A("G1", p=8), 0.0, eq, ks, mul)
-    if cfg["bitu"]:
-        iota(A("PR", p=1), [[0, 8], [64, 16]], 0, 0)
     ts(A("PJ", 0, 1), A("PI", 0, 1), 15, band); ts(A("PJ", 1, 2), A("PI", 0, 1), 3, band); ts(A("PJ", 2, 3), A("PI", 0, 1), 2, shr, 3, band)
     cp(col(0), A("PJ", 0, 1))
     ts(col(8), A("PJ", 1, 2), 16.0, mul); tt(col(7), col(8), A("PJ", 2, 3), add_)
     ts(A("PL"), A("IO", 0, 8), col(7), add_)
     cp(A("BL"), A("IO", 8, 16))
-    ts(col(1), col(0), 16.0, add_);
-    if not cfg["bitu"]:
-        ts(col(2), col(0), 64.0, mul)
+    ts(col(1), col(0), 16.0, add_); ts(col(2), col(0), 64.0, mul)
+    ts(A("LB", 0, 4), A("IO", 8, 12), 16.0, mul, col(2), add_)
     ts(col(4), col(0), 15.0, ALU.is_lt, HOLD, mul); ts(col(5), col(0), 4.0, mul); ts(col(6), col(0), 16.0, mul, float(ROT), add_)
     ts(A("B0"), A("IO", 8, 16), 64.0, mul, col(5), add_)
     ts(A("U3", 0, 8), A("IO", 8, 16), 256.0, mul, col(6), add_)
     ts(A("U4", 0, 8), A("U3", 0, 8), 2047, band); cp(A("BX", 8, 16), A("U4", 0, 8))
     cp(A("X", 2048, 2048 + OVER), A("X", 0, OVER)); ms(A("X", 2048 + OVER, 2064), 0.0)
     ms(A("MK"), 1.0); ms(A("MK", 0, 512, 16), 0.0)
-    ms(A("RB"), 0.0); ms(A("RB", 0, 64, 16), BIG)
+    ms(A("RB"), 1.0); ms(A("RB", 0, 64, 16), BIG)
     ms(A("F", 0, 16), 0.0); ms(A("DG", 0, 16), 0.0); ms(A("M128"), -136.0); ms(A("R32", p=1), 1.0 / 32)
     ms(A("SELP"), 0.0); ts(A("SELP", 15, 143, 16), A("B4", 0, 128, 16), 4 * ks, mul)
     if any(c[5] == "S" for c in cfg["chunks"]):
@@ -266,32 +265,27 @@ def build_ops(cfg):
     def index(t, h, b0, b1):
         c0, c1, J, ST, TT = 64 * h, 64 * h + 64, "J%d" % h, "ST%d" % t, "TT%d" % t
         one = A("ONE", p=1)
-        ab = A(ST, 256 + c0, 256 + c1, p=16)
+        ab = A(ST, 256 + c0, 256 + c1, p=18)
         tq = A(TT, c0, c1)
         x0, x1 = 64 * b0, 64 * b1
         qq = A("QQ", 192 * h + x0, 192 * h + x1)
         with_a = t > 0 and b1 == 3
         for bk in ("I1", J):
             end = bk == "I1"
-            rows = (0,) if end else (192, 384)
-            mm([(A(bk, x0, x1), one, A("CR", r + x0, r + x1, p=1), r < 384, False) for r in rows])
-            mm([(A(bk, 64 * b, 64 * b + 64), A(("SA", "SBB", "SD")[b], p=16), ab, False, False) for b in range(b0, b1)])
-            w = ("TA", "TB", "T3A" if end else "T3B")
+            s, w = ("SA", "SBB", "SD" if end else "SD2"), ("TA", "TB", "T3A" if end else "T3B")
+            mm([(A(bk, 64 * b, 64 * b + 64), A(s[b], p=18), ab, b == b0, False) for b in range(b0, b1)])
             mm([(A(bk, 64 * b, 64 * b + 64), A(w[b]), tq, False, end and not with_a and b == b1 - 1) for b in range(b0, b1)])
             if with_a:
                 mm([(A(bk, 64, 192), A("AR", p=1), A("Q4", p=1), False, end)])
             if end:
-                act(qq, A("I1", x0, x1), ACT.Identity, bias=127.5 + 1.0 / 512, scale=1.0 / 64)
+                act(qq, A("I1", x0, x1), ACT.Identity, bias=-0.5 + 1.0 / 512 - 1.125 / 64, scale=1.0 / 64)
         mm([(A(J, x0, x1), A("N64"), qq, False, True)])
         v0, v1 = 128 * h + x0, 128 * h + min(x1, 128)
         for b in range(b0, min(b1, 2)):
             tt(A("VI", 128 * h + 64 * b, 128 * h + 64 * b + 64), A(J, 64 * b, 64 * b + 64), A("NL%d" % t, c0, c1), mul)
         pl = A("PL", 0, (v1 - v0) // 16)
-        if cfg["bitu"]:
-            ts(A("OFF", v0, v1), IND(A("VI", v0, v1), pl), 2047, band)
-        else:
-            ts(A("VM", v0, v1), A("VI", v0, v1), 2047, band)
-            cp(A("OFF", v0, v1), IND(A("VM", v0, v1), pl))
+        ts(A("VM", v0, v1), A("VI", v0, v1), 2047, band)
+        cp(A("OFF", v0, v1), IND(A("VM", v0, v1), pl))
 
     def big(t, q):
         h, p0, p1, gf, gb, ce = cfg["chunks"][q]
@@ -312,25 +306,17 @@ def build_ops(cfg):
             act(A("MZ", n0, n1), A("AZ", n0, n1), ACT.Relu, bias=255.0, scale=-1.0)
         sel = "SELP" if ce == "V" else "SELN"
         dd = A("P%d" % h, 0, 64)
-        lst = [(dd, A("ONE", p=1), A("CR", 576, 640, p=1), True, False)] if p0 == 0 else []
-        if p0 == 0 and cfg["bitu"]:
-            lst.append((dd, A("PR", p=1), A("ONE", 0, 64, p=1), False, False))
-        for p in range(p0, p1):
-            lst.append((dd, A(sel, 15 - p, 143 - p), A("MZ", 1024 * h + 64 * p, 1024 * h + 64 * p + 64), False, p == 15))
-        mm(lst)
+        mm([(dd, A(sel, 15 - p, 143 - p), A("MZ", 1024 * h + 64 * p, 1024 * h + 64 * p + 64), p == 0, p == 15) for p in range(p0, p1)])
 
     def post(t, h, prev):
         c0, c1, l0, l1, P, J = 64 * h, 64 * h + 64, 4 * h, 4 * h + 4, "P%d" % h, "J%d" % h
         last = t == V - 1
-        key = A("KEY", c0 + 15, c1, 16)
+        key = A("KEY", c0, c1, 16)
         kk, ok = (A("KK", 0, 4), A("KK", 4, 8)) if h == 0 else (A("KK", 12, 16), A("KK", 8, 12))
         xk, xo = (A("XX", 0, 64), A("XX", 64, 128)) if h == 0 else (A("XX", 192, 256), A("XX", 128, 192))
-        scan(A("KEY", c0, c1), A("RB"), A(P, 0, 64), add_, mn)
-        ts(kk, key, 63, band)
-        if cfg["bitu"]:
-            ts(A("LK", l0, l1), key, 1023, band)
-        else:
-            ts(A("LK", l0, l1), kk, col(2), add_)
+        scan(A("KEY", c0, c1, -1), A("RB"), A(P, 0, 64, -1), add_, mn)
+        ts(kk, key, 15, band)
+        tt(A("LK", l0, l1), kk, A("LB", 0, 4), add_)
         tt(ok, key, A("THK", l0, l1), ALU.is_le)
         pf, room = IND(A("PF", 1024 * h, 1024 * h + 1024), A("LK", l0, l1)), A("ST%d" % t, 128 + c0, 128 + c1)
         tt(A("PM", c0, c1), pf, room, mn)
@@ -338,7 +324,7 @@ def build_ops(cfg):
         mm([(A(P, 128, 192), A("WM"), A("PM", c0, c1), False, True)])
         tt(A("XX", 128 * h, 128 * h + 128), IND(A("KK", 8 * h, 8 * h + 8), A("BL")), A("DG", 16, 144), mul)
         bc = A("CN", c0, c1)
-        mm([(bc, A("ONE", p=1), A("CR", 640, 704, p=1), True, False), (bc, A("B1"), xk, False, False), (bc, A("B16"), xo, False, True)])
+        mm([(bc, A("B1"), xk, True, False), (bc, A("B16"), xo, False, True)])
         if not last:
             mm([(A("P0", 256 + c0, 256 + c1, p=1), A("ONE", 0, 1), xo, True, True)])
             if h == 1:
@@ -347,11 +333,8 @@ def build_ops(cfg):
                 act(A("QA", p=1), A("R32", p=1), ACT.Identity, bias=-0.484375, scale=nc)
                 act(A("AR", p=1), A("QA", p=1), ACT.Identity, bias=nc, scale=-32.0)
         scan(A("HS", c0, c1), A("HM", 0, 64), A(P, 128, 192), add_, mn)
-        if cfg["bitu"]:
-            ts(A("LU", l0, l1), A("HS", c0 + 15, c1, 16), 511, band)
-        else:
-            ts(A("U5", l0, l1), A("HS", c0 + 15, c1, 16), 511, band)
-            cp(A("LU", l0, l1), A("U5", l0, l1))
+        ts(A("U5", l0, l1), A("HS", c0 + 15, c1, 16), 511, band)
+        cp(A("LU", l0, l1), A("U5", l0, l1))
         m2, dt, gm = A(J, 192, 256), A(J, 256, 320), A(J, 320, 384)
         ts(A("M1", c0, c1), bc, col(1), ALU.is_equal, 4.0, mul)
         w_m2 = ts(m2, bc, col(0), ALU.is_le)
@@ -525,11 +508,11 @@ def plan_waits(ops, queue, start):
 
 OPS = build_ops(CFG)
 ORDER = {
-    "V": "70 -59 54 -51 -1 60 -46 39 -50 12 -13 2 19 -4 2 3 -4 15 -5 4 -12 43 -28 -21 13 46 -5 15 -1 -23 -23 48 -53 -2 23 -15 -3 4 32 -29 13 54 -1 -38 40 -79 80 -25 4 5 30 -26 27 1 -87 1 80 -1 -28 30 14 -13 14 8 -51 -40 78 -35 45 4 1 -49 76 -17 18 2 -133 132 5 -3 -22 31 1 1 -5 6 -5 -18 19 -20 26 -40 41 -147 148 -32 38 -153 125 -122 -2 10 145 -154 8 147 2 -1 -4 9 -3 -5 17 -3 5 -4 16 -11 -4 2 4 10 -9 -227 45 183 9 15 -11 -194 192 -1 15 1 -14 25 -23 24 -23 24 17 -1 11 -9 10 -16 -1 2 1 9 10 3 29 -28 29 2 -1 5 -3 -31 40 -3 5 -4 5 -4 2 4 -36 37 -36 37 6 -34 1 -15 10 39 -29 30 1 1 2 -1 5 -3 30 -18 -3 5 -4 5 11 -15 2 18 -14 15 11 -25 9 17 -25 9 17 -16 27 -23 24 -23 24 17 -1 11 -9 10 -16 -1 2 1 9 13 -3 4 1 27 -17 18 2 -1 5 -3 -22 31 1 1 -5 6 -5 -19 20 -19 25 -40 41 7 -6 -32 39 -29 31 1 2 -1 5 -3 -5 17 -3 5 -4 5 -4 15 -13 4 15 -14 9 3 -11 9 15 -12 13 -15 4 12 -11 22 1 1 17 -1 11 -9 10 -16 -1 2 1 9 10 3 29 -28 29 2 -1 5 -3 -31 40 -3 5 -4 5 -4 2 4 -36 37 -36 37 -28 1 -15 48 -38 39 -29 30 1 1 2 -1 5 -3 29 1 -18 -3 5 11 -10 -5 3 29 -31 32 -26 27 -26 8 -7 8 1 27 -24 1 24 -23 24 17 -1 11 -9 10 -16 -1 2 1 9 13 -3 4 1 27 -17 18 2 -1 5 -3 -22 30 -3 -16 21 -4 -18 23 -4 2 -35 40 6 -5 -31 40 -30 31 1 1 -11 12 2 -1 5 -3 28 -20 -3 5 -4 5 -4 2 5 1 1 8 6 -1 2 -6 1 6 -5",
-    "S": "2 -1 -1 3 35 3 -2 1 49 -2 -6 9 -13 9 6 -17 1 41 -37 14 -12 11 -14 23 27 9 10 1 -53 49 13 -3 14 -62 61 10 1 -14 10 10 25 1 2 31 -1 -16 1 31 -30 17 25 23 10 1 -21 17 10 3 10 1 42 -32 -1 -13 45 -35 10 28 30 1 15 -32 1 18 -17 42 23 10 1 -21 17 10 3 11 -1 11 -1 -13 10 36 -26 25 3 30 1 -17 1 31 -13 -17 42 23 10 1 -21 17 10 3 10 11 -1 32 -41 -4 46 -36 10 28 30 -1 16 -31 1 17 -16 41 23 67 -57 1 -21 17 10 3 11 -1 11 -1 -13 48 -38 10 30 29 -1 -7 10 12 -1 2",
-    "P": "31 -1 100 -16 -23 27 -3 1 3 1 1 5 1 -26 27 3 -36 37 1 9 -37 38 1 8 -42 43 1 8 -15 10 15 -9 1 32 -3 1 3 -24 1 8 1 1 -17 10 10 25 44 1 51 -86 3 -2 3 72 -53 13 2 1 1 1 4 1 1 1 15 -13 1 1 1 1 4 6 13 -18 1 1 4 1 21 -9 -11 21 -7 10 5 94 1 -64 -21 24 -2 3 -34 1 9 1 8 1 1 28 -45 10 10 111 -76 86 -83 -2 3 32 -13 15 1 1 1 4 1 1 1 2 1 1 1 1 9 1 -6 19 -18 6 1 -6 1 26 -9 -11 21 8 -15 10 6 1 8 24 -3 1 3 -24 1 82 1 -75 1 1 -17 10 10 121 -96 86 -76 3 -2 3 19 15 1 1 -4 5 4 1 1 1 2 1 1 1 1 9 -5 1 18 -13 1 1 -6 1 26 -9 -11 21 -7 10 15 83 1 -63 -31 34 -2 3 -34 1 9 1 8 1 1 28 -45 10 10 120 -10 -75 3 -2 34 -31 33 1 1 1 -18 22 1 1 3 -2 3 1 1 1 4 1 4 14 -13 1 1 -6 1 26 -9 -11 21 8 -15 10 6 1 8 21 3 -2 -21 1 8 1 1 -17 47 -37 10 37 3 -2 20",
-    "G": "18 1 1 1 1 1 2 -1 2 77 102 4 28 4 1 119 4 28 4 1 119 4 28 4 1 119 4 28 4 118 5 26 5",
-    "Y": "4 1 1 1 1 1 1 823 1 45 -15 1",
+    "V": "11 55 -53 11 1 45 -49 1 24 -23 25 -4 5 -23 21 -20 40 -38 7 19 32 -53 -2 10 8 21 -38 2 50 -34 48 -62 61 -70 55 -26 -4 21 12 -28 42 -55 -2 16 46 17 -1 -69 12 20 39 -55 39 17 -51 -12 48 1 4 22 1 1 -37 -47 58 35 -75 -3 -7 -6 92 -35 -53 71 1 -57 58 -68 69 9 10 3 29 -28 29 2 -30 29 5 -3 -22 1 30 1 -4 5 -23 19 -33 38 -4 -19 25 8 -38 31 -21 22 -142 -51 202 -2 3 2 -1 5 -3 -5 17 -3 4 1 -4 16 -15 16 -12 15 -13 14 -13 10 13 -9 10 -13 14 -24 33 -19 20 -19 20 15 -1 11 -9 10 -17 1 1 1 9 10 3 29 -28 29 -28 30 -1 -19 24 -3 -22 31 -3 -32 33 3 1 -3 -20 1 25 -2 3 -31 32 -22 28 1 2 1 2 -1 5 -3 -5 17 -3 5 -4 16 -11 -4 19 -13 -4 14 4 -13 14 9 -13 14 -13 14 -24 14 19 1 1 14 1 10 -9 -36 46 -17 1 1 1 9 10 3 29 -28 31 -2 -28 29 5 -3 -22 1 30 -3 -18 22 1 -4 -33 34 4 -23 25 1 -31 32 -22 28 1 2 1 2 -1 5 -3 -5 17 -3 5 16 -20 5 -2 -2 15 -9 10 5 -1 -13 23 -13 14 -13 14 -24 33 -19 20 -19 20 15 -1 11 -9 10 -16 -1 2 1 9 10 3 29 -28 29 2 -30 29 5 -3 -22 1 30 -21 18 5 -4 5 -23 33 -12 -2 -34 40 -30 31 -21 22 7 2 1 2 -1 5 -3 29 -34 17 -3 5 -4 15 -10 -2 -2 19 -4 -9 10 -9 13 9 -12 13 -9 10 -23 32 -18 19 1 15 -1 11 -9 10 -17 1 1 1 9 10 3 1 28 -27 30 -2 -18 19 5 -3 -22 31 -4 3 -20 22 -4 -17 18 -33 40 -30 40 -30 17 4 10 2 -11 12 2 -1 5 -3 -5 13 -3 5 -4 5 -4 2 5 1 1 8 4 2 -1 2 -6 7 -6 1",
+    "S": "2 -1 -1 3 78 10 -11 8 -48 53 -11 -3 -38 49 -52 56 23 -39 17 -56 50 8 -20 26 -27 59 10 1 -19 15 10 -44 47 10 1 9 -13 14 -4 10 25 1 2 31 -1 -16 1 30 -29 17 22 20 10 1 -20 16 10 3 11 -1 -3 13 1 -4 10 26 -1 3 31 -1 -16 1 30 -12 -17 39 20 10 1 -20 16 10 3 10 1 9 -13 14 -4 10 26 -1 3 30 1 -17 1 30 -12 -17 39 20 10 1 -20 16 10 3 11 -1 10 1 -14 10 10 25 1 2 29 1 -16 1 29 -12 -16 38 87 -67 10 1 -20 16 10 3 11 -1 11 -1 -13 10 10 27 1 2 28 1 -8 10 12 -1 2",
+    "P": "30 1 61 23 1 2 1 1 -24 10 -4 37 -14 1 -15 38 -21 12 1 -12 21 -20 21 -7 10 5 1 1 32 -3 1 3 -25 1 1 8 1 1 -17 10 10 25 80 -70 3 -2 3 33 -3 1 45 -42 -15 20 1 -5 6 2 1 1 1 8 -4 5 1 -5 1 15 10 -9 -11 21 -7 10 5 1 1 32 -3 1 3 -25 1 1 8 1 1 -17 10 10 25 80 -33 -37 3 -2 3 76 -57 11 1 3 1 4 1 1 2 1 1 1 4 1 1 2 1 1 11 10 -9 -11 21 -7 10 5 1 1 32 -3 1 3 -25 1 1 8 1 1 -17 10 10 35 37 -47 80 -67 1 -3 79 -46 1 3 -15 20 1 -5 6 2 1 1 1 4 17 -16 1 2 1 1 21 -9 -11 21 -7 10 5 1 1 32 -3 1 3 -25 1 1 8 1 1 -17 10 10 114 -79 -10 14 -1 -2 68 -36 1 -12 20 1 -7 1 1 6 2 1 1 1 4 1 1 2 1 1 11 10 -9 -11 21 -7 10 5 1 1 32 -3 1 -22 1 1 8 1 1 -17 10 10 37 -10 13 -2 20",
+    "G": "15 -1 2 1 3 -2 1 85 98 4 28 4 1 113 4 28 4 1 113 4 28 4 1 113 4 28 4 112 5 26 5",
+    "Y": "4 1 1 1 1 1 1 796 1 45 -15 1",
 }
 if ORDER:
     QUEUE = {}
@@ -550,6 +533,9 @@ KIND = {o["sem"]: o["kind"] for o in OPS if o["sem"]}
 SEMAPHORES = ["eV", "eS", "eP", "eG", "sent"] + list(KIND)
 
 
+STEP = 1
+
+
 def rank_program(g, core, T, topo):
     rank = T.rank_of(core)
     if rank is None:
@@ -558,7 +544,7 @@ def rank_program(g, core, T, topo):
     arrive = {}
     for o in OPS:
         if o["kind"] == "r":
-            arrive[o["sem"]] = len(topo.engines(T.cores[(rank - o["dst"]) % N], core))
+            arrive[o["sem"]] = len(topo.engines(T.cores[(rank - o["dst"]) % N], core)[::STEP])
 
     def count(s, c):
         return c if s not in KIND else 16 if KIND[s] == "d" else arrive[s]
@@ -574,8 +560,9 @@ def rank_program(g, core, T, topo):
             if call == "remote":
                 d = T.cores[(rank + o["dst"]) % N]
                 rid, pid = topo.addr(d, core)
-                g.remote_dma(resolve(T, o["args"][0]), resolve(T, o["args"][1]), T.sem[o["sem"]], T.sem.sent, pid, rid, topo.mask(core, d))
-                sent += len(topo.engines(core, d))
+                g.remote_dma(resolve(T, o["args"][0]), resolve(T, o["args"][1]), T.sem[o["sem"]], T.sem.sent, pid, rid,
+                             sum(1 << x for x in topo.engines(core, d)[::STEP]))
+                sent += len(topo.engines(core, d)[::STEP])
                 continue
             if call == "mm":
                 for m in o["args"]:

@@ -1,47 +1,58 @@
+from concourse.bass import DstId, RemoteDMATransfer
 from concourse.mybir import AluOpType as ALU, ActivationFunctionType as ACT
 
 N, V = 8, 5
 ROT = 167
-OVER = ROT % 16
 NOFF = 148.0 + 2.0 ** -10
-BIG, HOLD = 2.0 ** 24, 2.0 ** 22
+BIG, TOP, LOW = 2.0 ** 24, 2.0 ** 22, 2.0 ** 21
+OKV = 512.0
+UW = 19
+QB = -33.0 / 64
 bf, f32, i32, u16 = "bfloat16", "float32", "int32", "uint16"
 
 SCRATCH = {}
 for _n, _c, _d in [
-        ("X", 2064, bf), ("C", 1024, f32), ("CI", 512, i32), ("CO", 512, f32), ("LI", 128, i32), ("TI", 128, i32), ("ABI", 128, i32),
-        ("EP", 128, bf), ("WI", 128, i32), ("WR", 128, bf), ("WM", 128, bf), ("THI", 128, i32), ("THF", 128, f32), ("THS", 128, f32),
-        ("THK", 8, f32), ("ONE", 128, bf), ("Q4", 128, bf), ("B4", 128, bf), ("TA", 128, bf), ("TB", 128, bf), ("T3A", 128, bf),
-        ("T3B", 128, bf), ("ID", 128, bf), ("NID", 128, bf), ("N64", 128, bf), ("B1", 128, bf), ("B16", 128, bf), ("SA", 128, bf),
-        ("SBB", 128, bf), ("SD", 128, bf), ("S8", 128, f32), ("PERM", 128, bf), ("E", 2048, bf), ("REP", 128, bf), ("DG", 144, bf),
-        ("HM", 128, bf), ("HM1", 128, bf), ("HM2", 128, bf), ("SELP", 144, bf), ("SELN", 144, bf), ("PI", 8, i32), ("PJ", 8, i32),
-        ("COL", 16, f32), ("IO", 16, i32), ("PL", 8, u16), ("BL", 8, u16), ("MK", 512, bf), ("RB", 64, bf), ("LB", 8, f32),
-        ("B0", 8, f32), ("BX", 16, f32), ("M128", 128, bf), ("R32", 128, f32),
-        ("F", 2064, bf), ("B", 2048, bf), ("PF", 2048, bf), ("SB", 2048, bf), ("AZ", 2048, bf), ("MZ", 2048, bf),
-        ("QQ", 384, bf), ("VI", 256, i32), ("VM", 256, i32), ("OFF", 256, u16), ("KEY", 128, i32), ("SP", 128, bf), ("KK", 16, i32),
-        ("LK", 8, u16), ("SD2", 128, bf), ("PM", 128, bf), ("XX", 256, bf), ("HS", 128, i32), ("NWM", 128, bf), ("U5", 8, i32),
-        ("LU", 8, u16), ("U2", 16, i32), ("U3", 16, i32), ("U4", 16, i32), ("LS", 16, u16), ("OK5", 8, f32), ("M1", 128, f32),
-        ("G1", 128, bf), ("G2", 128, bf), ("GL", 128, f32), ("W255", 64, bf), ("FK", 128, bf), ("FB", 128, bf), ("AV", 128, bf),
-        ("NC", 8, f32), ("CJ", 128, f32), ("QA", 128, bf), ("AR", 128, bf), ("LR", 128, f32),
-        ("FL", 128, f32), ("FT", 128, f32), ("OL", 128, f32), ("OT", 128, f32)]:
+        ("X", 2224, bf), ("C", 1024, f32), ("CI", 512, i32), ("CO", 1024, f32), ("LI", 128, i32), ("TI", 128, i32), ("ABI", 128, i32),
+        ("SP", 128, bf), ("EP", 128, bf), ("WI", 128, i32), ("WR", 128, bf), ("WM", 128, bf), ("NWM", 128, bf),
+        ("THI", 128, i32), ("THF", 128, f32), ("THS", 8 * UW, f32), ("THK", 8, f32), ("THE", 128, f32), ("ID32", 128, f32),
+        ("ONE", 128, bf), ("ONE32", 128, f32), ("Q64", 128, bf), ("TA", 128, bf), ("TB", 128, bf), ("T3A", 128, bf), ("T3B", 128, bf),
+        ("ID", 128, bf), ("NID", 128, bf), ("N64", 128, bf), ("B1", 128, bf), ("SA", 128, bf), ("SBB", 128, bf), ("SD", 128, bf),
+        ("SD2", 128, bf), ("S8", 128, f32), ("E", 1024, bf), ("EI", 1024, bf), ("IQ", 4 * UW, bf), ("OH", 4 * UW + 2, bf),
+        ("HT", 4 * UW, f32), ("H1", 4 * UW, f32), ("H2", 4 * UW, f32), ("H3", 4 * UW, f32), ("HA", 4 * UW, f32), ("HB", 4 * UW, f32),
+        ("CR", 4 * UW + 4, f32), ("MW", 544, bf), ("MN", 528, bf), ("SELP", 144, bf), ("PI", 8, i32), ("PJ", 8, i32), ("COL", 16, f32),
+        ("IO", 16, i32), ("PL", 8, u16), ("BL", 8, u16), ("MK", 512, bf), ("R0", 64, f32), ("R1", 64, f32), ("B0", 8, f32),
+        ("BX", 8, f32), ("M128", 128, bf), ("G1", 128, bf), ("G2", 128, bf), ("W255", 4 * UW, bf),
+        ("F", 2048, bf), ("B", 2048, bf), ("PF", 2048, bf), ("SB", 2048, bf), ("AZ", 2048, bf), ("MZ", 2048, bf),
+        ("QQ", 384, bf), ("DL", 128, bf), ("VI", 256, i32), ("VM", 256, i32), ("OFF", 256, u16), ("KEY", 128, i32), ("DM", 128, f32),
+        ("KK", 8, i32), ("OK", 8, bf), ("LK", 8, u16), ("LM", 8, u16), ("PM", 128, bf), ("U1", 8 * UW, i32), ("U2", 8 * UW, f32),
+        ("U3", 8 * UW, f32), ("U4", 8, i32), ("LU", 8, u16), ("LS", 16, u16), ("GL", 128, f32), ("MG", 128, bf), ("FK", 128, bf),
+        ("FB", 128, bf), ("AV", 128, bf), ("QA", 8, bf), ("BC", 8, f32), ("AR", 64, bf), ("LR", 128, f32), ("DT", 128, bf),
+        ("T32", 128, f32), ("FL", 128, f32), ("FT", 128, f32)]:
     SCRATCH[_n] = ("sbuf", [128, _c], _d)
 for _t in range(V):
     SCRATCH["NL%d" % _t] = ("sbuf", [128, 128], f32)
     SCRATCH["TT%d" % _t] = ("sbuf", [128, 128], bf)
     SCRATCH["ST%d" % _t] = ("sbuf", [128, 384], bf)
-for _t in range(V - 1):
-    SCRATCH["NO%d" % _t] = ("sbuf", [128, 128], f32)
-    SCRATCH["TO%d" % _t] = ("sbuf", [128, 128], bf)
+    SCRATCH["NO%d" % _t] = ("sbuf", [128, 256], f32)
+    SCRATCH["TO%d" % _t] = ("sbuf", [128, 128], bf if _t < V - 1 else f32)
 for _n in ("Z0", "Z1", "I1", "J0", "J1", "P0", "P1", "CN"):
     SCRATCH[_n] = ("psum", [128, 512], f32)
 
-CFG = {"chunks": [(0, 0, 8, "S", "V", "V"), (0, 8, 16, "S", "S", "V"), (1, 0, 7, "S", "V", "V"), (1, 7, 13, "S", "S", "V"), (1, 13, 16, "V", "S", "V")],
-       "ec": "S" * 9 + "V" * 7, "split": (1, 0), "bitu": False, "ttu": True, "xsplit": 1, "slack": 30, "bias": {},
-       "cv": 1.04, "g": 1.56, "sc": 3.8, "pe": 0.55, "lat": 90.0, "riss": 600.0, "rlat": 2600.0, "dlat": 2200.0}
+CFG = {"chunks": [(1, 0, 8, "S", "V", "V"), (1, 8, 16, "V", "S", "V"), (0, 0, 6, "S", "V", "V"), (0, 6, 12, "S", "S", "V"), (0, 12, 16, "V", "S", "V")],
+       "mode": "Y", "split": (0, 1), "joint": (1, 1), "nmask": "PP", "ar": "V", "over": "V", "cs": 0, "slack": 30, "bias": {},
+       "cv": 1.0, "g": 1.27, "sc": 2.8, "pe": 0.45, "lat": 200.0, "riss": 400.0, "rlat": 1700.0, "dlat": 1700.0}
+
+
+PART = {}
+for _n, _m in (("HB", "HA"), ("R1", "R0"), ("BL", "PL"), ("B0", "BX"), ("PJ", "PI"), ("T32", "LR"), ("HT", "HA"), ("DT", "MG")):
+    PART.setdefault(_m, (_m, 0, SCRATCH[_m][1][1]))
+    PART[_n] = (_m, SCRATCH[_m][1][1], SCRATCH[_n][1][1])
+    SCRATCH[_m][1][1] += SCRATCH.pop(_n)[1][1]
 
 
 def A(name, lo=0, hi=None, step=1, p=128, p0=0):
-    return ("A", name, lo, SCRATCH[name][1][1] if hi is None else hi, step, p0, p)
+    name, at, n = PART.get(name) or (name, 0, SCRATCH[name][1][1])
+    return ("A", name, at + lo, at + (n if hi is None else hi), step, p0, p)
 
 
 def IND(win, off):
@@ -71,13 +82,8 @@ def resolve(T, a):
     return T[name][p0:p, lo:hi:step]
 
 
-def place(o, eng):
-    o["eng"] = eng
-    o["call"], o["args"], o["kw"], o["dur"] = o["alt"][eng]
-
-
 def build_ops(cfg):
-    ops, acc, bank, now = [], {}, {}, [-1]
+    ops, acc, bank, now = [], {}, {}, [-1, "s"]
     cv = cfg["cv"]
 
     def add(eng, call, args, outs, ins, dur, kind="c", sem=None, lat=0.0, tag=None, after=(), kw=None, dst=0):
@@ -114,13 +120,12 @@ def build_ops(cfg):
             acc[name].append((lo, hi, i, wr, tag if wr else None))
         deps.discard(i)
         order.discard(i)
-        dur += cfg.get("ov" + eng, 0.0)
         ops.append({"eng": eng, "call": call, "args": args, "kw": kw or {}, "deps": deps, "order": order - deps, "dur": dur,
-                    "kind": kind, "sem": sem, "lat": lat, "dst": dst, "t": now[0]})
+                    "kind": kind, "sem": sem, "lat": lat, "dst": dst, "t": now[0], "sec": now[1]})
         return i
 
     def two(*aps):
-        return all(SCRATCH[a[1]][2] in (bf, u16) and SCRATCH[a[1]][0] == "sbuf" for a in aps)
+        return all(a[0] == "A" and SCRATCH[a[1]][2] in (bf, u16) and SCRATCH[a[1]][0] == "sbuf" for a in aps)
 
     def cost(o, ins, f):
         if o[0] == "I":
@@ -131,33 +136,28 @@ def build_ops(cfg):
 
     def ts(o, i, s1, a, s2=None, b=None, tag=None):
         args = [o, i, s1, s2, a] + ([] if b is None else [b])
-        return add("V", "tensor_scalar", args, [o], [i, s1, s2], cost(o, [i], 0.5 if i[0] == "A" and two(o, i) else 1.0), tag=tag)
+        return add("V", "tensor_scalar", args, [o], [i, s1, s2], cost(o, [i], 0.5 if two(o, i) else 1.0), tag=tag)
 
     def cp(o, i, tag=None):
-        return add("V", "tensor_copy", [o, i], [o], [i], cost(o, [i], 0.5 if i[0] == "A" and o[0] == "A" and two(o, i) else 1.0), tag=tag)
+        return add("V", "tensor_copy", [o, i], [o], [i], cost(o, [i], 0.5 if two(o, i) else 1.0), tag=tag)
 
     def tt(o, a, b, op):
         ps = any(x[0] == "A" and SCRATCH[x[1]][0] == "psum" for x in (a, b))
         return add("V", "tensor_tensor", [o, a, b, op], [o], [a, b], cost(o, [a], 1.0 if ps else 2.0))
 
-    def scan(o, d0, d1, op0, op1):
-        return add("V", "tensor_tensor_scan", [o, d0, d1, 0.0, op0, op1], [o], [d0, d1], cost(o, [d0], 0.5 if two(o, d0, d1) else 1.0))
+    def scan(o, d0, d1, op0, op1, first=0.0):
+        return add("V", "tensor_tensor_scan", [o, d0, d1, first, op0, op1], [o], [d0, d1], cost(o, [d0], 0.5 if two(o, d0, d1) else 1.0))
 
     def ms(o, c, tag=None):
         return add("V", "memset", [o, c], [o], [], cost(o, [o], 0.5 if two(o) else 1.0), tag=tag)
 
-    def act(o, i, func, bias=0.0, scale=1.0, accum=None, tag=None):
+    def act(o, i, func=ACT.Identity, bias=0.0, scale=1.0, tag=None):
         kw = {"bias": bias, "scale": scale}
-        if accum is not None:
-            kw["accum_out"] = accum
-        return add("S", "activation", [o, i, func], [o] + ([accum] if accum else []), [i, bias, scale], 20.0 + cost(o, [i], 1.0), kw=kw, tag=tag)
+        return add("S", "activation", [o, i, func], [o], [i, bias, scale], 20.0 + cost(o, [i], 1.0), kw=kw, tag=tag)
 
     def mm(lst):
         dur = 30.0 + sum(max(min(64, size(m[1])), size(m[2])) * (4 if SCRATCH[m[2][1]][2] == f32 else 1) for m in lst) * cfg["pe"]
         return add("P", "mm", lst, [m[0] for m in lst], [m[1] for m in lst] + [m[2] for m in lst], dur)
-
-    def aff(o, i, pat, op, base, cm):
-        return add("G", "affine_select", [o, i, pat, op, 0.0, base, cm], [o], [i], 190.0 + 2 * size(o) * cv)
 
     def iota(o, pat, base, cm):
         kw = {} if SCRATCH[o[1]][2] == i32 else {"allow_small_or_imprecise_dtypes": True}
@@ -166,307 +166,333 @@ def build_ops(cfg):
     def dma(eng, o, i, extra=0.0, tag=None):
         return add(eng, "dma_start", [o, i], [o], [i], 120.0, kind="d", sem="d%d" % len(ops), lat=cfg["dlat"] + extra, tag=tag)
 
-    def send(o, i, dst, extra=0.0, after=()):
-        return add("G", "remote", [o, i], [o], [i], cfg["riss"], kind="r", sem="r%d" % len(ops), lat=cfg["rlat"] + extra, dst=dst, after=after)
+    def send(o, srcs, dst, extra=0.0, after=()):
+        return add("G", "remote", [o] + srcs, [o], srcs, cfg["riss"], kind="r", sem="r%d" % len(ops), lat=cfg["rlat"] + extra, dst=dst, after=after)
 
-    def either(eng, o, i, tag=None):
-        k = cp(o, i, tag)
-        ops[k]["alt"] = {"V": ("tensor_copy", [o, i], {}, ops[k]["dur"]),
-                         "S": ("activation", [o, i, ACT.Identity], {"bias": 0.0, "scale": 1.0}, 20.0 + cfg.get("ovS", 0.0) + cost(o, [i], 1.0))}
-        place(ops[k], eng)
-        return k
+    def copy(eng, o, i, tag=None):
+        return cp(o, i, tag) if eng == "V" else act(o, i, tag=tag)
 
-    def gather(eng, o, win, off):
-        return either(eng, o, IND(win, off))
+    def col(k, p=128):
+        return A("COL", k, k + 1, p=p)
 
-    def col(k):
-        return A("COL", k, k + 1)
-
-    add_, sub, mul, mn = ALU.add, ALU.subtract, ALU.mult, ALU.min
+    add_, sub, mul, mn, mx, eq = ALU.add, ALU.subtract, ALU.mult, ALU.min, ALU.max, ALU.is_equal
     band, shr = ALU.bitwise_and, ALU.logical_shift_right
+    chunks = cfg["chunks"]
+    halves = (chunks[0][0], 1 - chunks[0][0])
+    ks = 16.0
+    xwin = (ROT // 16 * 16, 1024 + ROT // 16 * 16)
+
+    def blocks(bank_, lo, lhs, rhs, c0, stop):
+        mm([(A(bank_, lo + UW * c, lo + UW * c + 16), lhs, rhs(c0 + 16 * c, c0 + 16 * c + 16), False, stop and c == 3) for c in range(4)])
 
     dma("S", A("TI"), D("tn"))
     dma("S", A("ABI", p=8), D("aa"), tag="ab")
     dma("S", A("ABI", p0=8, p=16), D("bb"), tag="ab")
     dma("S", A("LI"), D("lg"))
-    dma("Y", A("X", ROT, 2048), D("xt", 0, 2048 - ROT), 1200.0)
+    dma("Y", A("X", ROT, 2048 + ROT), D("xt"), 1200.0)
     dma("Y", A("X", 0, ROT), D("xt", 2048 - ROT, 2048), 1200.0)
     dma("Y", A("SP"), D("sp"), 1200.0)
     dma("Y", A("EP"), D("ep"), 1200.0)
     dma("Y", A("WI", p=1), D("wt"), 1200.0)
     dma("Y", A("THI", p=8), D("th"), 1200.0)
     dma("Y", A("CI"), D("ct"), 1800.0)
-    ms(A("ONE"), 1.0); ms(A("Q4"), 0.25); ms(A("ST0", 256, 384), 1.0)
+    ms(A("ONE"), 1.0); ms(A("Q64", p=1), 64.0); ms(A("ONE32", p=1), 1.0); ms(A("ST0", 256, 384), 1.0)
     iota(A("PI", 0, 1), [[1, 1]], 0, 1)
     iota(A("G1", p=32), [[-1, 8], [0, 16]], 0, 1)
     iota(A("G2"), [[1, 128]], 0, -1)
     iota(A("IO", 0, 8), [[64, 2], [4, 4]], 0, 0)
-    aff(A("PERM"), A("ONE"), [[64, 2], [1, 16], [16, 4]], ALU.is_equal, 0, -1)
-    aff(A("REP", p=16), A("ONE", p=16), [[0, 8], [-1, 16]], ALU.is_equal, 0, 1)
     iota(A("IO", 8, 16), [[1, 8]], 0, 0)
-    eq = ALU.is_equal
-    ts(col(9), A("PI", 0, 1), 16.0, eq, 9280.0, mul); ts(col(10), A("PI", 0, 1), 17.0, eq, 1.125, mul); tt(col(9), col(9), col(10), add_)
-    c9 = A("COL", 9, 10, p=32)
+    iota(A("IQ"), [[0, 4], [1, UW]], 0, 0)
+    ts(col(9), A("PI", 0, 1), 16.0, eq, 9280.0, mul); ts(col(10), A("PI", 0, 1), 17.0, eq, 1.125, mul); tt(col(11), col(9), col(10), add_)
     ts(A("SA", p=32), A("G1", p=32), 0.0, eq, 0.25, mul); ts(A("SBB", p=32), A("G1", p=32), 8.0, eq, 0.25, mul)
-    ts(A("SBB", p=32), A("SBB", p=32), c9, add_)
-    tt(A("SD", p=32), A("SBB", p=32), A("SA", p=32), sub)
-    ts(A("SD2", p=32), A("SD", p=32), A("COL", 10, 11, p=32), sub)
-    ts(A("SA", p=32), A("SA", p=32), c9, add_)
+    tt(A("SD2", p=32), A("SBB", p=32), A("SA", p=32), sub)
     for z in ("Z0", "Z1"):
         mm([(A(z, 0, 128), A("SA", p=8), A("SA", p=8), True, True)])
+    ts(A("SD", p=32), A("SD2", p=32), col(11, 32), add_); ts(A("SD2", p=32), A("SD2", p=32), col(9, 32), add_)
+    ts(A("SBB", p=32), A("SBB", p=32), col(11, 32), add_); ts(A("SA", p=32), A("SA", p=32), col(11, 32), add_)
     for name, op, c in (("TA", ALU.is_ge, 4.0), ("TB", ALU.is_lt, -4.0), ("T3A", ALU.not_equal, -4.0)):
         ts(A(name), A("G2"), 0.0, op, c, mul)
         tt(A(name), A("Z0", 0, 128), A(name), mul)
-    for name, c in (("T3B", -4.0), ("B4", 4.0), ("B1", 16.0), ("B16", 256.0)):
-        act(A(name), A("Z1", 0, 128), ACT.Identity, scale=c)
-    ts(A("N64"), A("G2"), 0.0, eq, -64.0, mul); ts(A("ID"), A("G2"), 0.0, eq); ts(A("NID"), A("G2"), 0.0, eq, -1.0, mul)
-    ks = 16.0
+    for name, c in (("T3B", -4.0), ("B1", 16.0)):
+        act(A(name), A("Z1", 0, 128), scale=c)
+    ts(A("N64"), A("G2"), 0.0, eq, -64.0, mul)
+    act(A("ID"), A("N64"), scale=-1.0 / 64); act(A("NID"), A("N64"), scale=1.0 / 64); act(A("ID32"), A("N64"), scale=-1.0 / 64)
     ts(A("S8", p=8), A("G1", p=8), 0.0, eq, ks, mul)
     ts(A("PJ", 0, 1), A("PI", 0, 1), 15, band); ts(A("PJ", 1, 2), A("PI", 0, 1), 3, band); ts(A("PJ", 2, 3), A("PI", 0, 1), 2, shr, 3, band)
-    cp(col(0), A("PJ", 0, 1))
+    ts(A("PJ", 3, 4), A("PI", 0, 1), 63, band)
+    cp(col(0), A("PJ", 0, 1)); cp(col(3), A("PJ", 3, 4))
     ts(col(8), A("PJ", 1, 2), 16.0, mul); tt(col(7), col(8), A("PJ", 2, 3), add_)
     ts(A("PL"), A("IO", 0, 8), col(7), add_)
     cp(A("BL"), A("IO", 8, 16))
-    ts(col(1), col(0), 16.0, add_); ts(col(2), col(0), 64.0, mul)
-    ts(A("LB", 0, 4), A("IO", 8, 12), 16.0, mul, col(2), add_)
-    ts(col(4), col(0), 15.0, ALU.is_lt, HOLD, mul); ts(col(5), col(0), 4.0, mul); ts(col(6), col(0), 16.0, mul, float(ROT), add_)
+    act(col(2), col(0), scale=64.0, bias=TOP); act(col(5), col(0), scale=4.0); act(col(6), col(0), scale=-16.0, bias=float(xwin[0] - ROT))
     ts(A("B0"), A("IO", 8, 16), 64.0, mul, col(5), add_)
-    ts(A("U3", 0, 8), A("IO", 8, 16), 256.0, mul, col(6), add_)
-    ts(A("U4", 0, 8), A("U3", 0, 8), 2047, band); cp(A("BX", 8, 16), A("U4", 0, 8))
-    cp(A("X", 2048, 2048 + OVER), A("X", 0, OVER)); ms(A("X", 2048 + OVER, 2064), 0.0)
     ms(A("MK"), 1.0); ms(A("MK", 0, 512, 16), 0.0)
-    ms(A("RB"), 1.0); ms(A("RB", 0, 64, 16), BIG)
-    ms(A("F", 0, 16), 0.0); ms(A("DG", 0, 16), 0.0); ms(A("M128"), -136.0); ms(A("R32", p=1), 1.0 / 32)
-    ms(A("SELP"), 0.0); ts(A("SELP", 15, 143, 16), A("B4", 0, 128, 16), 4 * ks, mul)
-    if any(c[5] == "S" for c in cfg["chunks"]):
-        act(A("SELN"), A("SELP"), ACT.Identity, scale=-1.0)
-    for k in range(16):
-        either(cfg["ec"][k], A("E", k, 2048, 16), A("PERM"), tag="e")
-    mm([(A("P0", 0, 128), A("REP", p=16), A("REP", p=16), True, True)])
-    act(A("DG", 16, 144), A("P0", 0, 128), ACT.Identity)
-    act(A("HM1"), A("DG", 16, 144), ACT.Identity, scale=BIG); act(A("HM2"), A("DG", 15, 143), ACT.Identity, scale=-HOLD)
-    mm([(A("P0", 128, 256), A("ID"), A("HM1"), True, False), (A("P0", 128, 256), A("ID"), A("HM2"), False, True)])
-    act(A("HM"), A("P0", 128, 256), ACT.Identity)
+    ms(A("PF", 0, 2048, 64), 0.0)
+    ms(A("R0"), 0.0); ms(A("R0", 0, 64, 16), TOP)
+    ms(A("R1"), 1.0); ts(A("R1", 0, 64, 16), A("IO", 8, 12), 16.0, mul, col(2), add_)
+    ms(A("M128"), -136.0)
+    ms(A("SELP"), 0.0); ts(A("SELP", 15, 143, 16), A("B1", 0, 128, 16), ks, mul)
+    w = 4 * UW
+    ms(A("OH", 0, 2), 0.0); ts(A("OH", 2, w + 2), A("IQ"), col(0), eq)
+    act(A("HT"), A("OH", 2, w + 2), scale=BIG)
+    act(A("H1"), A("OH", 1, w + 1), scale=-LOW - 0.5); tt(A("H1"), A("H1"), A("HT"), add_)
+    for name, tmp, m in (("H2", "HA", 512.0), ("H3", "HB", 16.0)):
+        act(A(name), A("OH", 1, w + 1), scale=m / 2 - 2.0 ** 23 * m); act(A(tmp), A("OH", 0, w), scale=2.0 ** 23 * m - LOW - m)
+        tt(A(name), A(name), A("HT"), add_); tt(A(name), A(name), A(tmp), add_)
+    ts(A("H3", UW - 1, w, UW), A("IO", 8, 12), -256.0, mul, col(6), add_)
+    ts(A("CR", 0, w, p=1), A("IQ", p=1), 16.0, ALU.is_lt, 0.5 - LOW, mul); ms(A("CR", w, w + 1, p=1), -(24 + QB) * 256 * OKV)
+    ms(A("MW"), 0.0); ts(A("MW", 0, 16), A("IQ", 0, 16), col(0), ALU.is_le); ts(A("MW", 528, 544), A("IQ", 0, 16), col(0), eq)
+    if "P" in cfg["nmask"]:
+        ms(A("MN"), 1.0); ts(A("MN", 0, 16), A("IQ", 0, 16), col(0), ALU.is_gt)
+    for q in range(2):
+        iota(A("EI", 512 * q, 512 * q + 512), [[1, 8], [16, 4], [0, 16]], 8 * q, 0)
+        ts(A("E", 512 * q, 512 * q + 512), A("EI", 512 * q, 512 * q + 512), col(3), eq)
     cp(A("TT0"), A("TI")); cp(A("ST0", 256, 384, p=16), A("ABI", p=16)); ts(A("NL0"), A("LI"), NOFF, add_)
-    ts(A("ST0", 128, 256), A("SP"), -1.0, mul, 255.0, add_)
-    mm([(A("P1", 0, 128), A("SP"), A("ID"), True, False), (A("P1", 0, 128), A("EP"), A("NID"), False, True)])
-    act(A("ST0", 0, 128), A("P1", 0, 128), ACT.Identity)
-    last_send = send(A("ST1"), A("ST0"), 1, 1500.0)
+    act(A("ST0", 128, 256), A("SP"), scale=-1.0, bias=255.0)
+    mm([(A("Z1", 0, 128), A("SP"), A("ID"), True, False), (A("Z1", 0, 128), A("EP"), A("NID"), False, True)])
+    act(A("ST0", 0, 128), A("Z1", 0, 128))
+    last_send = send(A("ST1"), [A("ST0")], 1, 1500.0)
     cp(A("WR", p=1), A("WI", p=1))
     mm([(A("CN", 0, 128), A("WR", p=1), A("ONE", p=1), True, True)])
     tt(A("WM"), A("CN", 0, 128), A("B1"), mul)
-    act(A("NWM"), A("WM"), ACT.Identity, scale=-1.0); ms(A("W255"), 255.0)
+    act(A("NWM"), A("WM"), scale=-1.0); ms(A("W255"), 255.0)
     cp(A("THF", p=8), A("THI", p=8))
-    mm([(A("CN", 128, 256), A("S8", p=8), A("THF", p=8), True, True)])
-    scan(A("THS"), A("HM"), A("CN", 128, 256), add_, mn)
-    ts(A("THK"), A("THS", 15, 128, 16), col(4), add_, ks - 1 - 4080 * ks, add_)
+    for h in range(2):
+        mm([(A("CN", 128 + w * h, 128 + w * h + w), A("ONE32", p=1), A("CR", 0, w, p=1), h == 0, False)])
+        blocks("CN", 128 + w * h, A("S8", p=8), lambda a, b: A("THF", a, b, p=8), 64 * h, h == 1)
+    for h in range(2):
+        scan(A("THS", w * h, w * h + w), A("H1"), A("CN", 128 + w * h, 128 + w * h + w), add_, mn)
+    ts(A("THK"), A("THS", UW - 1, 2 * w, UW), 2 * LOW + ks, add_, -1.0, mul)
+    act(A("THE"), IND(A("THK"), A("BL")))
     ts(A("C", 0, 512), A("CI"), NOFF, add_)
 
     def index(t, h, b0, b1):
         c0, c1, J, ST, TT = 64 * h, 64 * h + 64, "J%d" % h, "ST%d" % t, "TT%d" % t
-        one = A("ONE", p=1)
-        ab = A(ST, 256 + c0, 256 + c1, p=18)
-        tq = A(TT, c0, c1)
-        x0, x1 = 64 * b0, 64 * b1
-        qq = A("QQ", 192 * h + x0, 192 * h + x1)
+        ab, tq = A(ST, 256 + c0, 256 + c1, p=18), A(TT, c0, c1)
         with_a = t > 0 and b1 == 3
-        for bk in ("I1", J):
-            end = bk == "I1"
-            s, w = ("SA", "SBB", "SD" if end else "SD2"), ("TA", "TB", "T3A" if end else "T3B")
-            mm([(A(bk, 64 * b, 64 * b + 64), A(s[b], p=18), ab, b == b0, False) for b in range(b0, b1)])
-            mm([(A(bk, 64 * b, 64 * b + 64), A(w[b]), tq, False, end and not with_a and b == b1 - 1) for b in range(b0, b1)])
-            if with_a:
-                mm([(A(bk, 64, 192), A("AR", p=1), A("Q4", p=1), False, end)])
-            if end:
-                act(qq, A("I1", x0, x1), ACT.Identity, bias=-0.5 + 1.0 / 512 - 1.125 / 64, scale=1.0 / 64)
-        mm([(A(J, x0, x1), A("N64"), qq, False, True)])
-        v0, v1 = 128 * h + x0, 128 * h + min(x1, 128)
-        for b in range(b0, min(b1, 2)):
-            tt(A("VI", 128 * h + 64 * b, 128 * h + 64 * b + 64), A(J, 64 * b, 64 * b + 64), A("NL%d" % t, c0, c1), mul)
-        pl = A("PL", 0, (v1 - v0) // 16)
-        ts(A("VM", v0, v1), A("VI", v0, v1), 2047, band)
-        cp(A("OFF", v0, v1), IND(A("VM", v0, v1), pl))
+        by_bias = with_a and b0 == 1
+
+        def sums(outs, last, stop, row):
+            s, w = ("SA", "SBB", last[0]), ("TA", "TB", last[1])
+            row = row and outs[-1][0] > 0
+            mm([(o, A(s[b], p=18), ab, n == 0, False) for n, (b, o) in enumerate(outs)])
+            mm([(o, A(w[b]), tq, False, stop and not row and b == outs[-1][0]) for b, o in outs])
+            if row:
+                mm([(o, A("Q64", p=1), A("AR", p=1), False, stop and b == outs[-1][0]) for b, o in outs if b > 0])
+
+        def qq(x0, x1):
+            return A("QQ", 192 * h + 64 * x0, 192 * h + 64 * x1)
+
+        if b0 == 0:
+            sums([(b, A("I1", 64 * b, 64 * b + 64)) for b in range(3)], ("SD", "T3A"), True, with_a)
+        act(qq(b0, b1), A("I1", 64 * b0, 64 * b1), bias=A("BC", 0, 1) if by_bias else QB, scale=1.0 / 64)
+        e = min(b1, 2)
+        J, j0 = ("P%d" % h, 256) if b0 == 1 else (J, 0)
+        sums([(b, A(J, j0 + 64 * b, j0 + 64 * b + 64)) for b in range(b0, b1)], ("SD2", "T3B"), False, with_a)
+        mm([(A(J, j0 + 64 * b0, j0 + 64 * b1), A("N64"), qq(b0, b1), False, True)])
+        for b in range(b0, e):
+            tt(A("VI", 128 * h + 64 * b, 128 * h + 64 * b + 64), A(J, j0 + 64 * b, j0 + 64 * b + 64), A("NL%d" % t, c0, c1), mul)
+        for x0, x1 in ([(b0, e)] if cfg["joint"][h] else [(b, b + 1) for b in range(b0, e)]):
+            v0, v1 = 128 * h + 64 * x0, 128 * h + 64 * x1
+            ts(A("VM", v0, v1), A("VI", v0, v1), 2047, band)
+            cp(A("OFF", v0, v1), IND(A("VM", v0, v1), A("PL", 0, (v1 - v0) // 16)))
+        if b1 == 3:
+            act(A("DL", c0, c1), A(J, j0 + 128, j0 + 192), scale=4.0)
+
+    zturn, zs = [0], ("Z0", "Z1", "CN")
 
     def big(t, q):
-        h, p0, p1, gf, gb, ce = cfg["chunks"][q]
-        n0, n1, Z = 1024 * h + 64 * p0, 1024 * h + 64 * p1, A("Z%d" % (q % 2), 0, 64 * (p1 - p0))
+        h, p0, p1, gf, gb, form = chunks[q]
+        n0, n1 = 1024 * h + 64 * p0, 1024 * h + 64 * p1
         o0, o1 = 128 * h + 4 * p0, 128 * h + 4 * p1
-        mk = A("MK", 0, n1 - n0)
-        gather(gf, A("F", 16 + n0, 16 + n1), A("X", 0, 2048), A("OFF", o0, o1))
-        gather(gb, A("B", n0, n1), A("X", 0, 2048), A("OFF", o0 + 64, o1 + 64))
-        scan(A("PF", n0, n1), A("F", 15 + n0, 15 + n1), mk, add_, mul)
-        scan(A("SB", n0, n1, -1), mk, A("B", n0, n1, -1), mul, add_)
-        mm([(Z, A("ST%d" % t, 0, 128), A("E", n0, n1), True, False)])
-        mm([(Z, A("ID"), A("PF", n0, n1), False, False)])
-        mm([(Z, A("ID"), A("SB", n0, n1), False, True)])
-        act(A("AZ", n0, n1), Z, ACT.Abs)
-        if ce == "V":
-            ts(A("MZ", n0, n1), A("AZ", n0, n1), 255.0, sub, 0.0, mn)
-        else:
-            act(A("MZ", n0, n1), A("AZ", n0, n1), ACT.Relu, bias=255.0, scale=-1.0)
-        sel = "SELP" if ce == "V" else "SELN"
+        copy(gf, A("F", n0, n1), IND(A("X", 0, 2048), A("OFF", o0, o1)))
+        copy(gb, A("B", n0, n1), IND(A("X", 0, 2048), A("OFF", o0 + 64, o1 + 64)))
+        scan(A("PF", n0 + 1, n1), A("F", n0, n1 - 1), A("MK", 1, n1 - n0), add_, mul)
+        scan(A("SB", n0, n1, -1), A("MK", 0, n1 - n0), A("B", n0, n1, -1), mul, add_)
         dd = A("P%d" % h, 0, 64)
-        mm([(dd, A(sel, 15 - p, 143 - p), A("MZ", 1024 * h + 64 * p, 1024 * h + 64 * p + 64), p == 0, p == 15) for p in range(p0, p1)])
+        if p0 == 0:
+            mm([(dd, A("ID32"), A("THE", 64 * h, 64 * h + 64), True, False)])
+
+        def differences():
+            z = A(zs[zturn[0] % 3], 0, n1 - n0)
+            zturn[0] += 1
+            mm([(z, A("ST%d" % t, 0, 128, p0=64 * h, p=64 * h + 64), A("E", 64 * p0, 64 * p1, p0=64 * h, p=64 * h + 64), True, False)])
+            mm([(z, A("ID"), A("PF", n0, n1), False, False)])
+            mm([(z, A("ID"), A("SB", n0, n1), False, True)])
+            return z
+
+        def fold(src, stop):
+            mm([(dd, A("SELP", 15 - p, 143 - p), A(src, 1024 * h + 64 * p, 1024 * h + 64 * p + 64), False, stop and p == 15) for p in range(p0, p1)])
+
+        if form == "V":
+            act(A("AZ", n0, n1), differences(), ACT.Abs)
+            ts(A("MZ", n0, n1), A("AZ", n0, n1), 255.0, mn)
+            fold("MZ", True)
+        else:
+            za, zb = differences(), differences()
+            act(A("AZ", n0, n1), za, ACT.Relu, scale=-1.0)
+            ts(A("MZ", n0, n1), zb, 0.0, mx, 255.0, mn)
+            fold("AZ", False)
+            fold("MZ", True)
 
     def post(t, h, prev):
-        c0, c1, l0, l1, P, J = 64 * h, 64 * h + 64, 4 * h, 4 * h + 4, "P%d" % h, "J%d" % h
+        c0, c1, l0, l1, P = 64 * h, 64 * h + 64, 4 * h, 4 * h + 4, "P%d" % h
         last = t == V - 1
-        key = A("KEY", c0, c1, 16)
-        kk, ok = (A("KK", 0, 4), A("KK", 4, 8)) if h == 0 else (A("KK", 12, 16), A("KK", 8, 12))
-        xk, xo = (A("XX", 0, 64), A("XX", 64, 128)) if h == 0 else (A("XX", 192, 256), A("XX", 128, 192))
-        scan(A("KEY", c0, c1, -1), A("RB"), A(P, 0, 64, -1), add_, mn)
+        key, dm, kk, ok, lm = A("KEY", c0, c1, 16), A("DM", c0, c1, 16), A("KK", l0, l1), A("OK", l0, l1), A("LM", l0, l1)
+        scan(A("KEY", c0, c1, -1), A(P, 0, 64, -1), A("R1", 0, 64, -1), mn, add_, TOP)
+        scan(A("DM", c0, c1, -1), A(P, 0, 64, -1), A("R0", 0, 64, -1), mn, add_, TOP)
+        tt(A("LK", l0, l1), key, dm, sub)
+        ts(ok, dm, TOP, ALU.is_lt, OKV, mul)
         ts(kk, key, 15, band)
-        tt(A("LK", l0, l1), kk, A("LB", 0, 4), add_)
-        tt(ok, key, A("THK", l0, l1), ALU.is_le)
-        pf, room = IND(A("PF", 1024 * h, 1024 * h + 1024), A("LK", l0, l1)), A("ST%d" % t, 128 + c0, 128 + c1)
-        tt(A("PM", c0, c1), pf, room, mn)
-        mm([(A(P, 128, 192), A("WM"), A("W255"), True, False), (A(P, 128, 192), A("NWM"), room, False, False)])
-        mm([(A(P, 128, 192), A("WM"), A("PM", c0, c1), False, True)])
-        tt(A("XX", 128 * h, 128 * h + 128), IND(A("KK", 8 * h, 8 * h + 8), A("BL")), A("DG", 16, 144), mul)
-        bc = A("CN", c0, c1)
-        mm([(bc, A("B1"), xk, True, False), (bc, A("B16"), xo, False, True)])
+        tt(lm, kk, ok, add_)
+        ST, u = "ST%d" % t, A(P, 128, 128 + w)
+        tt(A("PM", c0, c1), IND(A("PF", 1024 * h, 1024 * h + 1024), A("LK", l0, l1)), A(ST, 128 + c0, 128 + c1), mn)
+        mm([(u, A("ONE32", p=1), A("CR", 0, w, p=1), True, False), (u, A("WM"), A("W255"), False, False)])
+        blocks(P, 128, A("NWM"), lambda a, b: A(ST, a, b), 128 + c0, False)
+        blocks(P, 128, A("WM"), lambda a, b: A("PM", a, b), c0, True)
         if not last:
-            mm([(A("P0", 256 + c0, 256 + c1, p=1), A("ONE", 0, 1), xo, True, True)])
-            if h == 1:
-                nc = A("NC", 0, 1, p=1)
-                act(A("CJ", p=1), A("P0", 256, 384, p=1), ACT.Identity, bias=42.0, scale=-1.0, accum=nc)
-                act(A("QA", p=1), A("R32", p=1), ACT.Identity, bias=-0.484375, scale=nc)
-                act(A("AR", p=1), A("QA", p=1), ACT.Identity, bias=nc, scale=-32.0)
-        scan(A("HS", c0, c1), A("HM", 0, 64), A(P, 128, 192), add_, mn)
-        ts(A("U5", l0, l1), A("HS", c0 + 15, c1, 16), 511, band)
-        cp(A("LU", l0, l1), A("U5", l0, l1))
-        m2, dt, gm = A(J, 192, 256), A(J, 256, 320), A(J, 320, 384)
-        ts(A("M1", c0, c1), bc, col(1), ALU.is_equal, 4.0, mul)
-        w_m2 = ts(m2, bc, col(0), ALU.is_le)
-        w_dt = tt(dt, A(J, 128, 192), A("M1", c0, c1), mul)
-        to, no = (A("OT", c0, c1), A("OL", c0, c1)) if last else (A("TO%d" % t, c0, c1), A("NO%d" % t, c0, c1))
-        ops[tt(to, dt, A("TT%d" % t, c0, c1), add_)]["deps"].add(w_dt)
+            cn = A(zs[zturn[0] % 3], 0, 1)
+            if h == halves[1]:
+                mm([(cn, A("ONE32", p=1), A("CR", w, w + 1, p=1), True, False)]
+                   + [(cn, A("ONE"), A("OK", c, c + 1), False, False) for c in range(4 - l0, 8 - l0)])
+                mm([(cn, A("ONE"), A("OK", c, c + 1), False, c == l1 - 1) for c in range(l0, l1)])
+                act(A("QA", 0, 1), cn, scale=1.0 / (256 * OKV), bias=24 + QB - (6144 - 15.5) / 256)
+                act(A("BC", 0, 1), cn, scale=-1.0 / (256 * OKV), bias=A("QA", 0, 1))
+                if cfg["ar"] == "V":
+                    ts(A("AR", p=1), A("ONE", 0, 64, p=1), A("BC", 0, 1, p=1), mul, -QB, add_)
+                else:
+                    act(A("AR", p=1), A("ONE", 0, 64, p=1), scale=A("BC", 0, 1, p=1), bias=-QB)
+        us = [A(x, w * h + UW - 1, w * h + w, UW) for x in ("U1", "U2", "U3")]
+        for x, y in (("U1", "H1"), ("U2", "H2"), ("U3", "H3")):
+            scan(A(x, w * h, w * h + w), A(y), u, add_, mn)
+        tt(A("LU", l0, l1), us[0], us[1], sub)
+        tt(A("LS", 8 + l0, 8 + l1), us[0], us[2], sub)
         dst = N - (V - 1) if last else 1
-        s1 = send(A("FT" if last else "TT%d" % (t + 1), c0, c1), to, dst, after=[prev])
-        nl = A("NL%d" % t, c0, c1)
+        tq, to = A("TT%d" % t, c0, c1), A("TO%d" % t, c0, c1)
         if last:
-            act(A("LR", c0, c1), nl, ACT.Identity, bias=-NOFF)
-        tt(A("GL", c0, c1), IND(A("C", 0, 512), A("LU", l0, l1)), nl, sub)
-        w_gm = tt(gm, m2, A("GL", c0, c1), mul)
-        ops[w_gm]["deps"].add(w_m2)
-        ops[tt(no, gm, A("LR", c0, c1) if last else nl, add_)]["deps"].add(w_gm)
-        s2 = send(A("FL" if last else "NL%d" % (t + 1), c0, c1), no, dst, after=[s1])
+            act(A("T32", c0, c1), tq)
+            tq = A("T32", c0, c1)
+        tt(to, IND(A("MW", 16, 544), lm), A("DL", c0, c1), mul)
+        s1 = send(A("FT" if last else "TT%d" % (t + 1), c0, c1), [tq, to], dst, after=[prev])
+        nl, no = A("NL%d" % t, c0, c1), A("NO%d" % t, c0, c1)
+        keep = nl
+        if last:
+            keep = A("LR", c0, c1)
+            act(keep, nl, bias=-NOFF)
+        if cfg["nmask"][h] == "V":
+            tt(A("GL", c0, c1), IND(A("C", 0, 512), A("LU", l0, l1)), nl, sub)
+            tt(no, IND(A("MW", 0, 528), lm), A("GL", c0, c1), mul)
+        else:
+            act(A("MG", c0, c1), IND(A("MW", 0, 528), lm))
+            tt(A("NO%d" % t, 128 + c0, 128 + c1), IND(A("MN"), lm), keep, mul)
+            keep = A("NO%d" % t, 128 + c0, 128 + c1)
+            tt(no, IND(A("CO" if last else "C", 0, 512), A("LU", l0, l1)), A("MG", c0, c1), mul)
+        s2 = send(A("FL" if last else "NL%d" % (t + 1), c0, c1), [keep, no], dst, after=[s1])
         if last:
             dma("Y", D("yt", c0, c1), A("FT", c0, c1))
-            dma("Y", D("yl", c0, c1), A("FL", c0, c1))
+            dma("YS"[h == halves[1]], D("yl", c0, c1), A("FL", c0, c1))
         return s2
 
-    def records(h0, h1):
-        c0, c1, l0, l1 = 64 * h0, 64 * h1, 8 + 4 * h0, 8 + 4 * h1
-        for h in range(h0, h1):
-            n0, lk, av = 1024 * h, A("LK", 4 * h, 4 * h + 4), A("P%d" % h, 192, 256)
-            fk, bk = A("FK", 64 * h, 64 * h + 64), A("FB", 64 * h, 64 * h + 64)
-            gather("S", fk, A("F", 16 + n0, 1040 + n0), lk)
-            gather("S", bk, A("B", n0, n0 + 1024), lk)
-            mm([(av, A("ID"), fk, True, False), (av, A("ID"), bk, False, True)])
-            act(A("AV", 64 * h, 64 * h + 64), av, ACT.Identity, bias=135.75, scale=0.5)
-        ts(A("U2", l0, l1), A("HS", c0 + 15, c1, 16), 15, band)
-        tt(A("LS", l0, l1), A("U2", l0, l1), A("BX", l0, l1), add_)
-        tt(IND(A("X"), A("LS", l0, l1)), A("AV", c0, c1), A("M128", c0, c1), add_)
-        if h1 == 2:
-            cp(A("X", 0, OVER), A("X", 2048, 2048 + OVER))
+    def records(t, h):
+        c0, c1, l0, l1 = 64 * h, 64 * h + 64, 8 + 4 * h, 12 + 4 * h
+        n0, lk, av = 1024 * h, A("LK", 4 * h, 4 * h + 4), A("J%d" % h, 256, 320)
+        fk, bk = A("FK", c0, c1), A("FB", c0, c1)
+        act(fk, IND(A("F", n0, n0 + 1024), lk))
+        act(bk, IND(A("B", n0, n0 + 1024), lk))
+        mm([(av, A("ID"), fk, True, False), (av, A("ID"), bk, False, True)])
+        act(A("AV", c0, c1), av, bias=135.75, scale=0.5)
+        tt(IND(A("X", xwin[h], n0 + 1024 + ROT), A("LS", l0, l1)), A("AV", c0, c1), A("M128", c0, c1), add_)
+        if t == V - 1:
+            dma("YS"[h], D("yx", n0, n0 + 1024), A("X", n0 + ROT, n0 + 1024 + ROT), 600.0)
+        elif h == 1:
+            copy(cfg["over"], A("X", 0, ROT), A("X", 2048, 2048 + ROT))
 
     def controls(t):
-        ts(A("OK5"), A("KK", 4, 12), 512.0, mul)
-        tt(A("BX", 0, 8), A("OK5"), A("B0"), add_)
-        ts(A("U2", 0, 8), A("HS", 15, 128, 16), 3, band)
-        tt(A("LS", 0, 8), A("U2", 0, 8), A("BX", 0, 8), add_)
-        cp(IND(A("C"), A("LS", 0, 8)), A("NL%d" % t))
+        last = t == V - 1
+        tt(A("BX"), A("OK"), A("B0"), add_)
+        ts(A("U4"), A("U1", UW - 1, 2 * w, UW), 3, band)
+        tt(A("LS", 0, 8), A("U4"), A("BX"), add_)
+        cp(IND(A("CO" if last else "C"), A("LS", 0, 8)), A("LR" if last else "NL%d" % t))
+        if last:
+            dma("Y", D("yc"), A("CO", 0, 512), 600.0)
 
     for t in range(V):
         now[0] = t
-        for h in range(2):
-            if cfg["split"][h] and t > 0:
-                index(t, h, 0, 1); index(t, h, 1, 3)
+        zturn[0] = 0
+        for h in halves:
+            if cfg["split"][h]:
+                now[1] = "a%d" % h
+                index(t, h, 0, 1)
+                now[1] = "i%d" % h
+                index(t, h, 1, 3)
             else:
+                now[1] = "i%d" % h
                 index(t, h, 0, 3)
-        for q in range(len(cfg["chunks"])):
+        now[1] = "c"
+        if t == V - 1:
+            act(A("CO", 0, 512), A("C", 0, 512), bias=-NOFF)
+        for q in range(len(chunks)):
+            now[1] = "b%d" % q
             big(t, q)
-        last_send = post(t, 0, last_send)
-        if cfg["xsplit"]:
-            records(0, 1)
-        last_send = post(t, 1, last_send)
+        for h in halves:
+            now[1] = "p%d" % h
+            last_send = post(t, h, last_send)
+            now[1] = "r%d" % h
+            records(t, h)
+        now[1] = "c"
         if t + 2 < V:
-            last_send = send(A("ST%d" % (t + 2)), A("ST0"), t + 2, 1500.0, after=[last_send])
-        records(1 if cfg["xsplit"] else 0, 2)
+            last_send = send(A("ST%d" % (t + 2)), [A("ST0")], t + 2, 1500.0, after=[last_send])
         controls(t)
-    dma("Y", D("yx", 0, 2048 - ROT), A("X", ROT, 2048), 1200.0)
-    dma("S", D("yx", 2048 - ROT, 2048), A("X", 0, ROT))
-    act(A("CO"), A("C", 0, 512), ACT.Identity, bias=-NOFF)
-    dma("S", D("yc"), A("CO"), 600.0)
     return ops
 
 
-def label(o):
-    a, b = (o["args"][-1][0], o["args"][-1][2]) if o["call"] == "mm" else (o["args"][0], o["args"][0])
-    a = a[2] if a[0] == "I" else a
-
+def label2(o):
     def short(x):
-        return (x[1][:2] if x[1][:2] in ("NL", "TT", "ST", "NO", "TO") else x[1]) + "_" + str(x[2])
-    return o["eng"] + short(a) + (short(b) if o["call"] == "mm" else "s" if b[0] == "I" else "")
+        x = x[2] if x[0] == "I" else x
+        return x[1][:2] if x[1][:2] in ("NL", "TT", "ST", "NO", "TO") else x[1]
+    if o["call"] == "mm":
+        return "m" + short(o["args"][-1][2])
+    return short(o["args"][0]) + ("s" if o["args"][0][0] == "I" else "")
 
 
-def schedule(ops, cfg):
-    n = len(ops)
+def names(ops):
+    seen, out = {}, []
+    for o in ops:
+        l = o["sec"] + "." + label2(o)
+        seen[o["t"], l] = seen.get((o["t"], l), 0) + 1
+        out.append(l + ("" if seen[o["t"], l] == 1 else "#%d" % seen[o["t"], l]))
+    return out
+
+
+def follow(ops, cfg, order):
+    rank = {}
+    for k, w in enumerate(order):
+        rank[w.lstrip("+-")] = k + len(order) * (w.count("-") - w.count("+"))
+    key, last = [], 0
+    for o, l in zip(ops, names(ops)):
+        last = rank.get(l, last)
+        key.append(max(o["t"], 0) * len(order) + last)
     succ = [[] for _ in ops]
+    left = [len(o["deps"] | o["order"]) for o in ops]
     for i, o in enumerate(ops):
         for j in o["deps"] | o["order"]:
             succ[j].append(i)
-    lat = cfg["lat"]
-    prio = [0.0] * n
-    for i in range(n - 1, -1, -1):
+    ready = [i for i in range(len(ops)) if not left[i]]
+    queue, free = {e: [] for e in "VSPGY"}, {e: 0.0 for e in "VSPGY"}
+    start, done = [0.0] * len(ops), [0.0] * len(ops)
+    while ready:
+        i = min(ready, key=lambda k: (key[k], k))
+        ready.remove(i)
         o = ops[i]
-        prio[i] = o["dur"] + o["lat"] + max([prio[k] + lat for k in succ[i]] + [0.0])
-    bias = cfg.get("bias", {})
-    prio = [x + bias.get(label(o), 0.0) for x, o in zip(prio, ops)]
-    left = [len(o["deps"] | o["order"]) for o in ops]
-    ready = {e: [] for e in "VSPGY"}
-    at = [0.0] * n
-    for i, o in enumerate(ops):
-        if left[i] == 0:
-            ready[o["eng"]].append(i)
-    free = {e: 0.0 for e in "VSPGY"}
-    queue = {e: [] for e in "VSPGY"}
-    start, done = [0.0] * n, [0.0] * n
-    slack = cfg.get("slack", 60.0)
-    for _ in range(n):
-        e = min((x for x in "VSPGY" if ready[x]), key=lambda x: max(free[x], min(at[i] for i in ready[x])))
-        t0 = max(free[e], min(at[i] for i in ready[e]))
-        i = max((k for k in ready[e] if at[k] <= t0 + slack), key=lambda k: (prio[k], -k))
-        ready[e].remove(i)
-        o = ops[i]
-        start[i] = max(free[e], at[i])
-        free[e] = start[i] + o["dur"]
-        done[i] = free[e] + o["lat"]
-        queue[e].append(i)
+        start[i] = max([free[o["eng"]]] + [done[j] + cfg["lat"] for j in o["deps"]])
+        free[o["eng"]] = start[i] + o["dur"]
+        done[i] = free[o["eng"]] + o["lat"]
+        queue[o["eng"]].append(i)
         for k in succ[i]:
-            at[k] = max(at[k], done[i] + lat if i in ops[k]["deps"] else start[i])
             left[k] -= 1
-            if left[k] == 0:
-                ready[ops[k]["eng"]].append(k)
+            if not left[k]:
+                ready.append(k)
     return queue, start, done
-
-
-def timed(ops, queue, cfg):
-    start, done = [None] * len(ops), [None] * len(ops)
-    at, free, left = {e: 0 for e in queue}, {e: 0.0 for e in queue}, len(ops)
-    while left:
-        before = left
-        for e, q in queue.items():
-            while at[e] < len(q) and all(done[j] is not None for j in ops[q[at[e]]]["deps"]):
-                i = q[at[e]]
-                start[i] = max([free[e]] + [done[j] + cfg["lat"] for j in ops[i]["deps"]])
-                free[e] = start[i] + ops[i]["dur"]
-                done[i] = free[e] + ops[i]["lat"]
-                at[e] += 1
-                left -= 1
-        assert left < before
-    return start, done
 
 
 def plan_waits(ops, queue, start):
@@ -506,34 +532,16 @@ def plan_waits(ops, queue, start):
     return mark, waits, rest
 
 
+ORDER = "s.X".split()
+ORDER6 = ORDER = """
+s.THF -r0.yx s.ST#5 s.ST#4 -p1.yl -c.yc i1.VI a1.VM i0.mST ++++++++++++++++++++b2.mSB b2.mPF i0.mST#2 b3.AZ s.E#2 i0.mTT -r0.LSs s.mONE a1.OFF i1.VM s.PL#2 b1.mE b0.mE i0.mTT#2 b5.B b1.mSB b1.F s.WM i1.OFF b5.F b0.F i0.QQ s.mTHF#2 b1.PF s.H1#2 s.mCR#2 b0.PF s.mTHF s.R0 s.mCR b2.mE i0.mQQ b0.SB s.SELP#2 b1.B -p0.yl b1.mPF b3.mPF s.H3 -p0.yt i0.mAR#2 b0.mPF b2.F -c.ST +b0.mSB s.COL#9 p1.MG b5.mE b3.mTHE b2.mMZ p0.LR#2 p0.LR ++i1.mQQ -c.BX s.NWM b2.B i0.VI s.THS#2 b1.SB i0.VI#2 b2.SB s.HA#3 s.HA#2 s.H2 s.M128 s.THS s.THE b2.PF b0.AZ b0.mTHE -c.LS +b4.F i0.VM b1.AZ s.H3#2 s.THK s.W255 b2.AZ i0.OFF s.H2#2 s.MW b0.mMZ b0.MZ b1.MZ b3.F s.R0#3 b1.mMZ b2.MZ s.H2#3 s.R0#2 s.R0#4 b3.PF b4.PF p1.mW255 p1.KEY s.MW#3 p1.mPM p1.DM b3.SB p1.OK p1.LK b5.mPF +b5.mSB p1.KK b4.SB p1.LM p1.PM +b3.B p1.mST b5.SB p1.TO b5.AZ b5.PF s.C c.CO +s.ONE s.MN ++b3.mSB r1.AV +a1.mST s.MW#2 -c.LSs p1.U1 +s.CI p1.TT +s.MK +s.ONE32 p0.mOK p1.FT p1.U2 s.MN#2 s.CR#2 b4.mMZ ++b5.mMZ +s.G1 b3.MZ +s.PF +s.WI +s.ABI +s.EP +b4.mSB +s.PI +s.ABI#2 b4.MZ +s.ST p1.LU +s.T3B +s.SBB +s.SA +s.COL +s.PI#4 +s.COL#2 +s.PI#2 +s.mSA p0.TT +s.G2 p0.mPM b3.mMZ +s.SD2 +s.TI +s.LI +s.SP +s.mSA#2 +s.IO +s.THI +s.X#2 p1.NL p1.NO +s.X b5.MZ +s.COL#3 +s.PI#3 +s.T3A +s.TA +b4.B p0.QA +s.B1 r1.mFB +a1.mTT#2 p1.NO#2 p0.mST +s.MK#2 +s.TB +s.N64 i0.DL s.H3#3 r1.FB +s.TA#2 +s.COL#6 p0.DM +s.TB#2 +s.PI#5 +s.SBB#2 r0.FK p0.KEY +s.ID p1.yt r1.FK +i1.mAR p1.FL s.H3#4 r0.FB +s.SA#2 s.BX p0.AR +s.COL#4 p0.OK +s.T3A#2 +b4.mE p0.KK +b3.mE p0.LK +s.ST#2 +s.SD +s.TT +s.NL s.Q64 p0.mOK#2 p1.U3 p0.LM p0.PM +s.IQ p1.LS p0.NL p0.TO p0.U1 r1.LSs p0.mW255 p0.U2 p0.NO +b4.mPF +s.EI +s.COL#7 +a1.QQ p0.BC p0.LU +s.ID32 p0.MG c.U4 +i1.DL p0.FT p0.U3 +a1.mTT +i1.mST +a1.mST#2 +p1.LR r0.mFB +s.OH#2 +s.CR +i1.QQ +s.EI#2 r0.AV r1.X +s.COL#5 +s.H1 +s.PL +s.NID +s.SD2#2 +s.COL#8 p0.FL +a1.mQQ +s.S8 +b4.AZ p0.NO#2 +s.WR +i1.mTT +s.HA +s.OH +s.E +a1.VI r1.yx +s.COL#10 p0.LS +b0.B +s.IO#2 +s.ST#3 +i0.mAR +s.SELP +s.mNID +p1.LR#2
+""".split()
+CFG.update(ar="V", over="S", chunks=[(1, 0, 7, 'V', 'S', 'V'), (1, 7, 12, 'S', 'S', 'V'), (1, 12, 16, 'S', 'V', 'V'), (0, 0, 7, 'V', 'S', 'V'), (0, 7, 13, 'S', 'S', 'V'), (0, 13, 16, 'S', 'S', 'V')])
 OPS = build_ops(CFG)
-ORDER = {
-    "V": "11 55 -53 11 1 45 -49 1 24 -23 25 -4 5 -23 21 -20 40 -38 7 19 32 -53 -2 10 8 21 -38 2 50 -34 48 -62 61 -70 55 -26 -4 21 12 -28 42 -55 -2 16 46 17 -1 -69 12 20 39 -55 39 17 -51 -12 48 1 4 22 1 1 -37 -47 58 35 -75 -3 -7 -6 92 -35 -53 71 1 -57 58 -68 69 9 10 3 29 -28 29 2 -30 29 5 -3 -22 1 30 1 -4 5 -23 19 -33 38 -4 -19 25 8 -38 31 -21 22 -142 -51 202 -2 3 2 -1 5 -3 -5 17 -3 4 1 -4 16 -15 16 -12 15 -13 14 -13 10 13 -9 10 -13 14 -24 33 -19 20 -19 20 15 -1 11 -9 10 -17 1 1 1 9 10 3 29 -28 29 -28 30 -1 -19 24 -3 -22 31 -3 -32 33 3 1 -3 -20 1 25 -2 3 -31 32 -22 28 1 2 1 2 -1 5 -3 -5 17 -3 5 -4 16 -11 -4 19 -13 -4 14 4 -13 14 9 -13 14 -13 14 -24 14 19 1 1 14 1 10 -9 -36 46 -17 1 1 1 9 10 3 29 -28 31 -2 -28 29 5 -3 -22 1 30 -3 -18 22 1 -4 -33 34 4 -23 25 1 -31 32 -22 28 1 2 1 2 -1 5 -3 -5 17 -3 5 16 -20 5 -2 -2 15 -9 10 5 -1 -13 23 -13 14 -13 14 -24 33 -19 20 -19 20 15 -1 11 -9 10 -16 -1 2 1 9 10 3 29 -28 29 2 -30 29 5 -3 -22 1 30 -21 18 5 -4 5 -23 33 -12 -2 -34 40 -30 31 -21 22 7 2 1 2 -1 5 -3 29 -34 17 -3 5 -4 15 -10 -2 -2 19 -4 -9 10 -9 13 9 -12 13 -9 10 -23 32 -18 19 1 15 -1 11 -9 10 -17 1 1 1 9 10 3 1 28 -27 30 -2 -18 19 5 -3 -22 31 -4 3 -20 22 -4 -17 18 -33 40 -30 40 -30 17 4 10 2 -11 12 2 -1 5 -3 -5 13 -3 5 -4 5 -4 2 5 1 1 8 4 2 -1 2 -6 7 -6 1",
-    "S": "2 -1 -1 3 78 10 -11 8 -48 53 -11 -3 -38 49 -52 56 23 -39 17 -56 50 8 -20 26 -27 59 10 1 -19 15 10 -44 47 10 1 9 -13 14 -4 10 25 1 2 31 -1 -16 1 30 -29 17 22 20 10 1 -20 16 10 3 11 -1 -3 13 1 -4 10 26 -1 3 31 -1 -16 1 30 -12 -17 39 20 10 1 -20 16 10 3 10 1 9 -13 14 -4 10 26 -1 3 30 1 -17 1 30 -12 -17 39 20 10 1 -20 16 10 3 11 -1 10 1 -14 10 10 25 1 2 29 1 -16 1 29 -12 -16 38 87 -67 10 1 -20 16 10 3 11 -1 11 -1 -13 10 10 27 1 2 28 1 -8 10 12 -1 2",
-    "P": "30 1 61 23 1 2 1 1 -24 10 -4 37 -14 1 -15 38 -21 12 1 -12 21 -20 21 -7 10 5 1 1 32 -3 1 3 -25 1 1 8 1 1 -17 10 10 25 80 -70 3 -2 3 33 -3 1 45 -42 -15 20 1 -5 6 2 1 1 1 8 -4 5 1 -5 1 15 10 -9 -11 21 -7 10 5 1 1 32 -3 1 3 -25 1 1 8 1 1 -17 10 10 25 80 -33 -37 3 -2 3 76 -57 11 1 3 1 4 1 1 2 1 1 1 4 1 1 2 1 1 11 10 -9 -11 21 -7 10 5 1 1 32 -3 1 3 -25 1 1 8 1 1 -17 10 10 35 37 -47 80 -67 1 -3 79 -46 1 3 -15 20 1 -5 6 2 1 1 1 4 17 -16 1 2 1 1 21 -9 -11 21 -7 10 5 1 1 32 -3 1 3 -25 1 1 8 1 1 -17 10 10 114 -79 -10 14 -1 -2 68 -36 1 -12 20 1 -7 1 1 6 2 1 1 1 4 1 1 2 1 1 11 10 -9 -11 21 -7 10 5 1 1 32 -3 1 -22 1 1 8 1 1 -17 10 10 37 -10 13 -2 20",
-    "G": "15 -1 2 1 3 -2 1 85 98 4 28 4 1 113 4 28 4 1 113 4 28 4 1 113 4 28 4 112 5 26 5",
-    "Y": "4 1 1 1 1 1 1 796 1 45 -15 1",
-}
-if ORDER:
-    QUEUE = {}
-    for _e, _s in ORDER.items():
-        QUEUE[_e] = []
-        for _w in _s.split():
-            QUEUE[_e].append((QUEUE[_e][-1] if QUEUE[_e] else 0) + int(_w))
-        for _i in QUEUE[_e]:
-            if _i < len(OPS) and "alt" in OPS[_i] and _e in "VS":
-                place(OPS[_i], _e)
-    if sorted(i for q in QUEUE.values() for i in q) != list(range(len(OPS))) or any(OPS[i]["eng"] != e for e, q in QUEUE.items() for i in q):
-        QUEUE = schedule(OPS, CFG)[0]
-else:
-    QUEUE = schedule(OPS, CFG)[0]
-START, DONE = timed(OPS, QUEUE, CFG)
+QUEUE, START, DONE = follow(OPS, CFG, ORDER)
 MARK, WAITS, REST = plan_waits(OPS, QUEUE, START)
 KIND = {o["sem"]: o["kind"] for o in OPS if o["sem"]}
 SEMAPHORES = ["eV", "eS", "eP", "eG", "sent"] + list(KIND)
-
-
-STEP = 1
 
 
 def rank_program(g, core, T, topo):
@@ -544,7 +552,7 @@ def rank_program(g, core, T, topo):
     arrive = {}
     for o in OPS:
         if o["kind"] == "r":
-            arrive[o["sem"]] = len(topo.engines(T.cores[(rank - o["dst"]) % N], core)[::STEP])
+            arrive[o["sem"]] = len(topo.engines(T.cores[(rank - o["dst"]) % N], core))
 
     def count(s, c):
         return c if s not in KIND else 16 if KIND[s] == "d" else arrive[s]
@@ -560,9 +568,14 @@ def rank_program(g, core, T, topo):
             if call == "remote":
                 d = T.cores[(rank + o["dst"]) % N]
                 rid, pid = topo.addr(d, core)
-                g.remote_dma(resolve(T, o["args"][0]), resolve(T, o["args"][1]), T.sem[o["sem"]], T.sem.sent, pid, rid,
-                             sum(1 << x for x in topo.engines(core, d)[::STEP]))
-                sent += len(topo.engines(core, d)[::STEP])
+                a = [resolve(T, x) for x in o["args"]]
+                if len(a) == 2:
+                    g.remote_dma(a[0], a[1], T.sem[o["sem"]], T.sem.sent, pid, rid, topo.mask(core, d))
+                else:
+                    g.remote_dma_fused([RemoteDMATransfer(dst_ids=[DstId(rid=rid, pnc=pid)], dma_engine_mask=topo.mask(core, d),
+                                                          remote_sem=T.sem[o["sem"]], srcs=a[1:], dsts=a[:1], alu_op=1)],
+                                       local_sem=T.sem.sent)
+                sent += len(topo.engines(core, d))
                 continue
             if call == "mm":
                 for m in o["args"]:
@@ -576,7 +589,6 @@ def rank_program(g, core, T, topo):
                 elif call == "tensor_tensor_scan": ins = eng.tensor_tensor_scan(*a)
                 elif call == "memset": ins = eng.memset(*a)
                 elif call == "activation": ins = eng.activation(*a, **kw)
-                elif call == "affine_select": ins = eng.affine_select(*a)
                 elif call == "iota": ins = eng.iota(*a, **kw)
                 else: ins = eng.dma_start(*a)
             s = MARK[i][0]

from concourse.bass import DstId, RemoteDMATransfer
from concourse.mybir import AluOpType as ALU, ActivationFunctionType as ACT

N, V = 8, 5
ROT = 167
NOFF = 148.0 + 2.0 ** -10
BIG, TOP, LOW = 2.0 ** 24, 2.0 ** 22, 2.0 ** 21
OKV = 512.0
UW = 19
QB = -33.0 / 64
bf, f32, i32, u16 = "bfloat16", "float32", "int32", "uint16"

SCRATCH = {}
for _n, _c, _d in [
        ("X", 2224, bf), ("C", 1024, f32), ("CI", 512, i32), ("CO", 1024, f32), ("LI", 128, i32), ("TI", 128, i32), ("ABI", 128, i32),
        ("SP", 128, bf), ("EP", 128, bf), ("WI", 128, i32), ("WR", 128, bf), ("WM", 128, bf), ("NWM", 128, bf),
        ("THI", 128, i32), ("THF", 128, f32), ("THS", 8 * UW, f32), ("THK", 8, f32), ("THE", 128, f32), ("ID32", 128, f32),
        ("ONE", 128, bf), ("ONE32", 128, f32), ("Q64", 128, bf), ("TA", 128, bf), ("TB", 128, bf), ("T3A", 128, bf), ("T3B", 128, bf),
        ("ID", 128, bf), ("NID", 128, bf), ("N64", 128, bf), ("B1", 128, bf), ("SA", 128, bf), ("SBB", 128, bf), ("SD", 128, bf),
        ("SD2", 128, bf), ("S8", 128, f32), ("E", 1024, bf), ("EI", 1024, bf), ("IQ", 4 * UW, bf), ("OH", 4 * UW + 2, bf),
        ("HT", 4 * UW, f32), ("H1", 4 * UW, f32), ("H2", 4 * UW, f32), ("H3", 4 * UW, f32), ("HA", 4 * UW, f32), ("HB", 4 * UW, f32),
        ("CR", 4 * UW + 4, f32), ("MW", 544, bf), ("MN", 528, bf), ("SELP", 144, bf), ("PI", 8, i32), ("PJ", 8, i32), ("COL", 16, f32),
        ("IO", 16, i32), ("PL", 8, u16), ("BL", 8, u16), ("MK", 512, bf), ("R0", 64, f32), ("R1", 64, f32), ("B0", 8, f32),
        ("BX", 8, f32), ("M128", 128, bf), ("G1", 128, bf), ("G2", 128, bf), ("W255", 4 * UW, bf),
        ("F", 2048, bf), ("B", 2048, bf), ("PF", 2048, bf), ("SB", 2048, bf), ("AZ", 2048, bf), ("MZ", 2048, bf),
        ("QQ", 384, bf), ("DL", 128, bf), ("VI", 256, i32), ("VM", 256, i32), ("OFF", 256, u16), ("KEY", 128, i32), ("DM", 128, f32),
        ("KK", 8, i32), ("OK", 8, bf), ("LK", 8, u16), ("LM", 8, u16), ("PM", 128, bf), ("U1", 8 * UW, i32), ("U2", 8 * UW, f32),
        ("U3", 8 * UW, f32), ("U4", 8, i32), ("LU", 8, u16), ("LS", 16, u16), ("GL", 128, f32), ("MG", 128, bf), ("FK", 128, bf),
        ("FB", 128, bf), ("AV", 128, bf), ("QA", 8, bf), ("BC", 8, f32), ("AR", 64, bf), ("LR", 128, f32), ("DT", 128, bf),
        ("T32", 128, f32), ("FL", 128, f32), ("FT", 128, f32)]:
    SCRATCH[_n] = ("sbuf", [128, _c], _d)
for _t in range(V):
    SCRATCH["NL%d" % _t] = ("sbuf", [128, 128], f32)
    SCRATCH["TT%d" % _t] = ("sbuf", [128, 128], bf)
    SCRATCH["ST%d" % _t] = ("sbuf", [128, 384], bf)
    SCRATCH["NO%d" % _t] = ("sbuf", [128, 256], f32)
    SCRATCH["TO%d" % _t] = ("sbuf", [128, 128], bf if _t < V - 1 else f32)
for _n in ("Z0", "Z1", "I1", "J0", "J1", "P0", "P1", "CN"):
    SCRATCH[_n] = ("psum", [128, 512], f32)

CFG = {"chunks": [(1, 0, 8, "S", "V", "V"), (1, 8, 16, "V", "S", "V"), (0, 0, 6, "S", "V", "V"), (0, 6, 12, "S", "S", "V"), (0, 12, 16, "V", "S", "V")],
       "mode": "Y", "split": (0, 1), "joint": (1, 1), "nmask": "PP", "ar": "V", "over": "V", "cs": 0, "slack": 30, "bias": {},
       "cv": 1.0, "g": 1.27, "sc": 2.8, "pe": 0.45, "lat": 200.0, "riss": 400.0, "rlat": 1700.0, "dlat": 1700.0}


PART = {}
for _n, _m in (("HB", "HA"), ("R1", "R0"), ("BL", "PL"), ("B0", "BX"), ("PJ", "PI"), ("T32", "LR"), ("HT", "HA"), ("DT", "MG")):
    PART.setdefault(_m, (_m, 0, SCRATCH[_m][1][1]))
    PART[_n] = (_m, SCRATCH[_m][1][1], SCRATCH[_n][1][1])
    SCRATCH[_m][1][1] += SCRATCH.pop(_n)[1][1]


def A(name, lo=0, hi=None, step=1, p=128, p0=0):
    name, at, n = PART.get(name) or (name, 0, SCRATCH[name][1][1])
    return ("A", name, at + lo, at + (n if hi is None else hi), step, p0, p)


def IND(win, off):
    return ("I", win, off)


def D(name, lo=None, hi=None):
    return ("D", name, lo, hi)


def size(a):
    return (a[3] - a[2] + abs(a[4]) - 1) // abs(a[4])


def resolve(T, a):
    if not isinstance(a, tuple):
        return a
    if a[0] == "I":
        return resolve(T, a[1]).indirect(resolve(T, a[2]))
    if a[0] == "D":
        return T[a[1]][:] if a[2] is None else T[a[1]][:, a[2]:a[3]]
    _, name, lo, hi, step, p0, p = a
    if step == 1:
        return T[name][p0:p, lo:hi]
    if step == -1:
        return T[name][p0:p, hi - 1::-1] if lo == 0 else T[name][p0:p, hi - 1:lo - 1:-1]
    return T[name][p0:p, lo:hi:step]


def build_ops(cfg):
    ops, acc, bank, now = [], {}, {}, [-1, "s"]
    cv = cfg["cv"]

    def add(eng, call, args, outs, ins, dur, kind="c", sem=None, lat=0.0, tag=None, after=(), kw=None, dst=0):
        i = len(ops)
        deps, order = set(), set(after)
        items = []
        for a, wr in [(x, True) for x in outs] + [(x, False) for x in ins]:
            if not isinstance(a, tuple) or a[0] == "D":
                continue
            if a[0] == "I":
                items += [(a[1], wr), (a[2], False)]
            else:
                items.append((a, wr))
        for a, wr in items:
            name, lo, hi = a[1], a[2], a[3]
            if SCRATCH[name][0] == "psum":
                st = bank.setdefault(name, [None, [], []])
                if st[0] != eng:
                    st[0], st[2], st[1] = eng, st[1], []
                deps.update(st[2])
                if eng == "P":
                    order.update(st[1])
                st[1].append(i)
                continue
            for (l2, h2, j, w2, t2) in acc.setdefault(name, []):
                if l2 < hi and lo < h2 and (wr or w2) and not (tag is not None and t2 == tag):
                    deps.add(j)
        for a, wr in items:
            name, lo, hi = a[1], a[2], a[3]
            if SCRATCH[name][0] == "psum":
                continue
            if wr and abs(a[4]) == 1 and a[5] == 0 and a[6] == 128:
                acc[name] = [e for e in acc[name] if not (lo <= e[0] and e[1] <= hi)]
            acc[name].append((lo, hi, i, wr, tag if wr else None))
        deps.discard(i)
        order.discard(i)
        ops.append({"eng": eng, "call": call, "args": args, "kw": kw or {}, "deps": deps, "order": order - deps, "dur": dur,
                    "kind": kind, "sem": sem, "lat": lat, "dst": dst, "t": now[0], "sec": now[1]})
        return i

    def two(*aps):
        return all(a[0] == "A" and SCRATCH[a[1]][2] in (bf, u16) and SCRATCH[a[1]][0] == "sbuf" for a in aps)

    def cost(o, ins, f):
        if o[0] == "I":
            return 55.0 + size(ins[0]) * cfg["sc"] * cv
        if ins[0][0] == "I":
            return 55.0 + size(o) * cfg["g"] * cv
        return max(64.0, size(o) * f) * cv

    def ts(o, i, s1, a, s2=None, b=None, tag=None):
        args = [o, i, s1, s2, a] + ([] if b is None else [b])
        return add("V", "tensor_scalar", args, [o], [i, s1, s2], cost(o, [i], 0.5 if two(o, i) else 1.0), tag=tag)

    def cp(o, i, tag=None):
        return add("V", "tensor_copy", [o, i], [o], [i], cost(o, [i], 0.5 if two(o, i) else 1.0), tag=tag)

    def tt(o, a, b, op):
        ps = any(x[0] == "A" and SCRATCH[x[1]][0] == "psum" for x in (a, b))
        return add("V", "tensor_tensor", [o, a, b, op], [o], [a, b], cost(o, [a], 1.0 if ps else 2.0))

    def scan(o, d0, d1, op0, op1, first=0.0):
        return add("V", "tensor_tensor_scan", [o, d0, d1, first, op0, op1], [o], [d0, d1], cost(o, [d0], 0.5 if two(o, d0, d1) else 1.0))

    def ms(o, c, tag=None):
        return add("V", "memset", [o, c], [o], [], cost(o, [o], 0.5 if two(o) else 1.0), tag=tag)

    def act(o, i, func=ACT.Identity, bias=0.0, scale=1.0, tag=None):
        kw = {"bias": bias, "scale": scale}
        return add("S", "activation", [o, i, func], [o], [i, bias, scale], 20.0 + cost(o, [i], 1.0), kw=kw, tag=tag)

    def mm(lst):
        dur = 30.0 + sum(max(min(64, size(m[1])), size(m[2])) * (4 if SCRATCH[m[2][1]][2] == f32 else 1) for m in lst) * cfg["pe"]
        return add("P", "mm", lst, [m[0] for m in lst], [m[1] for m in lst] + [m[2] for m in lst], dur)

    def iota(o, pat, base, cm):
        kw = {} if SCRATCH[o[1]][2] == i32 else {"allow_small_or_imprecise_dtypes": True}
        return add("G", "iota", [o, pat, base, cm], [o], [], 150.0 + 2 * size(o) * cv, kw=kw)

    def dma(eng, o, i, extra=0.0, tag=None):
        return add(eng, "dma_start", [o, i], [o], [i], 120.0, kind="d", sem="d%d" % len(ops), lat=cfg["dlat"] + extra, tag=tag)

    def send(o, srcs, dst, extra=0.0, after=()):
        return add("G", "remote", [o] + srcs, [o], srcs, cfg["riss"], kind="r", sem="r%d" % len(ops), lat=cfg["rlat"] + extra, dst=dst, after=after)

    def copy(eng, o, i, tag=None):
        return cp(o, i, tag) if eng == "V" else act(o, i, tag=tag)

    def col(k, p=128):
        return A("COL", k, k + 1, p=p)

    add_, sub, mul, mn, mx, eq = ALU.add, ALU.subtract, ALU.mult, ALU.min, ALU.max, ALU.is_equal
    band, shr = ALU.bitwise_and, ALU.logical_shift_right
    chunks = cfg["chunks"]
    halves = (chunks[0][0], 1 - chunks[0][0])
    ks = 16.0
    xwin = (ROT // 16 * 16, 1024 + ROT // 16 * 16)

    def blocks(bank_, lo, lhs, rhs, c0, stop):
        mm([(A(bank_, lo + UW * c, lo + UW * c + 16), lhs, rhs(c0 + 16 * c, c0 + 16 * c + 16), False, stop and c == 3) for c in range(4)])

    dma("S", A("TI"), D("tn"))
    dma("S", A("ABI", p=8), D("aa"), tag="ab")
    dma("S", A("ABI", p0=8, p=16), D("bb"), tag="ab")
    dma("S", A("LI"), D("lg"))
    dma("Y", A("X", ROT, 2048 + ROT), D("xt"), 1200.0)
    dma("Y", A("X", 0, ROT), D("xt", 2048 - ROT, 2048), 1200.0)
    dma("Y", A("SP"), D("sp"), 1200.0)
    dma("Y", A("EP"), D("ep"), 1200.0)
    dma("Y", A("WI", p=1), D("wt"), 1200.0)
    dma("Y", A("THI", p=8), D("th"), 1200.0)
    dma("Y", A("CI"), D("ct"), 1800.0)
    ms(A("ONE"), 1.0); ms(A("Q64", p=1), 64.0); ms(A("ONE32", p=1), 1.0); ms(A("ST0", 256, 384), 1.0)
    iota(A("PI", 0, 1), [[1, 1]], 0, 1)
    iota(A("G1", p=32), [[-1, 8], [0, 16]], 0, 1)
    iota(A("G2"), [[1, 128]], 0, -1)
    iota(A("IO", 0, 8), [[64, 2], [4, 4]], 0, 0)
    iota(A("IO", 8, 16), [[1, 8]], 0, 0)
    iota(A("IQ"), [[0, 4], [1, UW]], 0, 0)
    ts(col(9), A("PI", 0, 1), 16.0, eq, 9280.0, mul); ts(col(10), A("PI", 0, 1), 17.0, eq, 1.125, mul); tt(col(11), col(9), col(10), add_)
    ts(A("SA", p=32), A("G1", p=32), 0.0, eq, 0.25, mul); ts(A("SBB", p=32), A("G1", p=32), 8.0, eq, 0.25, mul)
    tt(A("SD2", p=32), A("SBB", p=32), A("SA", p=32), sub)
    for z in ("Z0", "Z1"):
        mm([(A(z, 0, 128), A("SA", p=8), A("SA", p=8), True, True)])
    ts(A("SD", p=32), A("SD2", p=32), col(11, 32), add_); ts(A("SD2", p=32), A("SD2", p=32), col(9, 32), add_)
    ts(A("SBB", p=32), A("SBB", p=32), col(11, 32), add_); ts(A("SA", p=32), A("SA", p=32), col(11, 32), add_)
    for name, op, c in (("TA", ALU.is_ge, 4.0), ("TB", ALU.is_lt, -4.0), ("T3A", ALU.not_equal, -4.0)):
        ts(A(name), A("G2"), 0.0, op, c, mul)
        tt(A(name), A("Z0", 0, 128), A(name), mul)
    for name, c in (("T3B", -4.0), ("B1", 16.0)):
        act(A(name), A("Z1", 0, 128), scale=c)
    ts(A("N64"), A("G2"), 0.0, eq, -64.0, mul)
    act(A("ID"), A("N64"), scale=-1.0 / 64); act(A("NID"), A("N64"), scale=1.0 / 64); act(A("ID32"), A("N64"), scale=-1.0 / 64)
    ts(A("S8", p=8), A("G1", p=8), 0.0, eq, ks, mul)
    ts(A("PJ", 0, 1), A("PI", 0, 1), 15, band); ts(A("PJ", 1, 2), A("PI", 0, 1), 3, band); ts(A("PJ", 2, 3), A("PI", 0, 1), 2, shr, 3, band)
    ts(A("PJ", 3, 4), A("PI", 0, 1), 63, band)
    cp(col(0), A("PJ", 0, 1)); cp(col(3), A("PJ", 3, 4))
    ts(col(8), A("PJ", 1, 2), 16.0, mul); tt(col(7), col(8), A("PJ", 2, 3), add_)
    ts(A("PL"), A("IO", 0, 8), col(7), add_)
    cp(A("BL"), A("IO", 8, 16))
    act(col(2), col(0), scale=64.0, bias=TOP); act(col(5), col(0), scale=4.0); act(col(6), col(0), scale=-16.0, bias=float(xwin[0] - ROT))
    ts(A("B0"), A("IO", 8, 16), 64.0, mul, col(5), add_)
    ms(A("MK"), 1.0); ms(A("MK", 0, 512, 16), 0.0)
    ms(A("PF", 0, 2048, 64), 0.0)
    ms(A("R0"), 0.0); ms(A("R0", 0, 64, 16), TOP)
    ms(A("R1"), 1.0); ts(A("R1", 0, 64, 16), A("IO", 8, 12), 16.0, mul, col(2), add_)
    ms(A("M128"), -136.0)
    ms(A("SELP"), 0.0); ts(A("SELP", 15, 143, 16), A("B1", 0, 128, 16), ks, mul)
    w = 4 * UW
    ms(A("OH", 0, 2), 0.0); ts(A("OH", 2, w + 2), A("IQ"), col(0), eq)
    act(A("HT"), A("OH", 2, w + 2), scale=BIG)
    act(A("H1"), A("OH", 1, w + 1), scale=-LOW - 0.5); tt(A("H1"), A("H1"), A("HT"), add_)
    for name, tmp, m in (("H2", "HA", 512.0), ("H3", "HB", 16.0)):
        act(A(name), A("OH", 1, w + 1), scale=m / 2 - 2.0 ** 23 * m); act(A(tmp), A("OH", 0, w), scale=2.0 ** 23 * m - LOW - m)
        tt(A(name), A(name), A("HT"), add_); tt(A(name), A(name), A(tmp), add_)
    ts(A("H3", UW - 1, w, UW), A("IO", 8, 12), -256.0, mul, col(6), add_)
    ts(A("CR", 0, w, p=1), A("IQ", p=1), 16.0, ALU.is_lt, 0.5 - LOW, mul); ms(A("CR", w, w + 1, p=1), -(24 + QB) * 256 * OKV)
    ms(A("MW"), 0.0); ts(A("MW", 0, 16), A("IQ", 0, 16), col(0), ALU.is_le); ts(A("MW", 528, 544), A("IQ", 0, 16), col(0), eq)
    if "P" in cfg["nmask"]:
        ms(A("MN"), 1.0); ts(A("MN", 0, 16), A("IQ", 0, 16), col(0), ALU.is_gt)
    for q in range(2):
        iota(A("EI", 512 * q, 512 * q + 512), [[1, 8], [16, 4], [0, 16]], 8 * q, 0)
        ts(A("E", 512 * q, 512 * q + 512), A("EI", 512 * q, 512 * q + 512), col(3), eq)
    cp(A("TT0"), A("TI")); cp(A("ST0", 256, 384, p=16), A("ABI", p=16)); ts(A("NL0"), A("LI"), NOFF, add_)
    act(A("ST0", 128, 256), A("SP"), scale=-1.0, bias=255.0)
    mm([(A("Z1", 0, 128), A("SP"), A("ID"), True, False), (A("Z1", 0, 128), A("EP"), A("NID"), False, True)])
    act(A("ST0", 0, 128), A("Z1", 0, 128))
    last_send = send(A("ST1"), [A("ST0")], 1, 1500.0)
    cp(A("WR", p=1), A("WI", p=1))
    mm([(A("CN", 0, 128), A("WR", p=1), A("ONE", p=1), True, True)])
    tt(A("WM"), A("CN", 0, 128), A("B1"), mul)
    act(A("NWM"), A("WM"), scale=-1.0); ms(A("W255"), 255.0)
    cp(A("THF", p=8), A("THI", p=8))
    for h in range(2):
        mm([(A("CN", 128 + w * h, 128 + w * h + w), A("ONE32", p=1), A("CR", 0, w, p=1), h == 0, False)])
        blocks("CN", 128 + w * h, A("S8", p=8), lambda a, b: A("THF", a, b, p=8), 64 * h, h == 1)
    for h in range(2):
        scan(A("THS", w * h, w * h + w), A("H1"), A("CN", 128 + w * h, 128 + w * h + w), add_, mn)
    ts(A("THK"), A("THS", UW - 1, 2 * w, UW), 2 * LOW + ks, add_, -1.0, mul)
    act(A("THE"), IND(A("THK"), A("BL")))
    ts(A("C", 0, 512), A("CI"), NOFF, add_)

    def index(t, h, b0, b1):
        c0, c1, J, ST, TT = 64 * h, 64 * h + 64, "J%d" % h, "ST%d" % t, "TT%d" % t
        ab, tq = A(ST, 256 + c0, 256 + c1, p=18), A(TT, c0, c1)
        with_a = t > 0 and b1 == 3
        by_bias = with_a and b0 == 1

        def sums(outs, last, stop, row):
            s, w = ("SA", "SBB", last[0]), ("TA", "TB", last[1])
            row = row and outs[-1][0] > 0
            mm([(o, A(s[b], p=18), ab, n == 0, False) for n, (b, o) in enumerate(outs)])
            mm([(o, A(w[b]), tq, False, stop and not row and b == outs[-1][0]) for b, o in outs])
            if row:
                mm([(o, A("Q64", p=1), A("AR", p=1), False, stop and b == outs[-1][0]) for b, o in outs if b > 0])

        def qq(x0, x1):
            return A("QQ", 192 * h + 64 * x0, 192 * h + 64 * x1)

        if b0 == 0:
            sums([(b, A("I1", 64 * b, 64 * b + 64)) for b in range(3)], ("SD", "T3A"), True, with_a)
        act(qq(b0, b1), A("I1", 64 * b0, 64 * b1), bias=A("BC", 0, 1) if by_bias else QB, scale=1.0 / 64)
        e = min(b1, 2)
        J, j0 = ("P%d" % h, 256) if b0 == 1 else (J, 0)
        sums([(b, A(J, j0 + 64 * b, j0 + 64 * b + 64)) for b in range(b0, b1)], ("SD2", "T3B"), False, with_a)
        mm([(A(J, j0 + 64 * b0, j0 + 64 * b1), A("N64"), qq(b0, b1), False, True)])
        for b in range(b0, e):
            tt(A("VI", 128 * h + 64 * b, 128 * h + 64 * b + 64), A(J, j0 + 64 * b, j0 + 64 * b + 64), A("NL%d" % t, c0, c1), mul)
        for x0, x1 in ([(b0, e)] if cfg["joint"][h] else [(b, b + 1) for b in range(b0, e)]):
            v0, v1 = 128 * h + 64 * x0, 128 * h + 64 * x1
            ts(A("VM", v0, v1), A("VI", v0, v1), 2047, band)
            cp(A("OFF", v0, v1), IND(A("VM", v0, v1), A("PL", 0, (v1 - v0) // 16)))
        if b1 == 3:
            act(A("DL", c0, c1), A(J, j0 + 128, j0 + 192), scale=4.0)

    zturn, zs = [0], ("Z0", "Z1", "CN")

    def big(t, q):
        h, p0, p1, gf, gb, form = chunks[q]
        n0, n1 = 1024 * h + 64 * p0, 1024 * h + 64 * p1
        o0, o1 = 128 * h + 4 * p0, 128 * h + 4 * p1
        copy(gf, A("F", n0, n1), IND(A("X", 0, 2048), A("OFF", o0, o1)))
        copy(gb, A("B", n0, n1), IND(A("X", 0, 2048), A("OFF", o0 + 64, o1 + 64)))
        scan(A("PF", n0 + 1, n1), A("F", n0, n1 - 1), A("MK", 1, n1 - n0), add_, mul)
        scan(A("SB", n0, n1, -1), A("MK", 0, n1 - n0), A("B", n0, n1, -1), mul, add_)
        dd = A("P%d" % h, 0, 64)
        if p0 == 0:
            mm([(dd, A("ID32"), A("THE", 64 * h, 64 * h + 64), True, False)])

        def differences():
            z = A(zs[zturn[0] % 3], 0, n1 - n0)
            zturn[0] += 1
            mm([(z, A("ST%d" % t, 0, 128, p0=64 * h, p=64 * h + 64), A("E", 64 * p0, 64 * p1, p0=64 * h, p=64 * h + 64), True, False)])
            mm([(z, A("ID"), A("PF", n0, n1), False, False)])
            mm([(z, A("ID"), A("SB", n0, n1), False, True)])
            return z

        def fold(src, stop):
            mm([(dd, A("SELP", 15 - p, 143 - p), A(src, 1024 * h + 64 * p, 1024 * h + 64 * p + 64), False, stop and p == 15) for p in range(p0, p1)])

        if form == "V":
            act(A("AZ", n0, n1), differences(), ACT.Abs)
            ts(A("MZ", n0, n1), A("AZ", n0, n1), 255.0, mn)
            fold("MZ", True)
        else:
            za, zb = differences(), differences()
            act(A("AZ", n0, n1), za, ACT.Relu, scale=-1.0)
            ts(A("MZ", n0, n1), zb, 0.0, mx, 255.0, mn)
            fold("AZ", False)
            fold("MZ", True)

    def post(t, h, prev):
        c0, c1, l0, l1, P = 64 * h, 64 * h + 64, 4 * h, 4 * h + 4, "P%d" % h
        last = t == V - 1
        key, dm, kk, ok, lm = A("KEY", c0, c1, 16), A("DM", c0, c1, 16), A("KK", l0, l1), A("OK", l0, l1), A("LM", l0, l1)
        scan(A("KEY", c0, c1, -1), A(P, 0, 64, -1), A("R1", 0, 64, -1), mn, add_, TOP)
        scan(A("DM", c0, c1, -1), A(P, 0, 64, -1), A("R0", 0, 64, -1), mn, add_, TOP)
        tt(A("LK", l0, l1), key, dm, sub)
        ts(ok, dm, TOP, ALU.is_lt, OKV, mul)
        ts(kk, key, 15, band)
        tt(lm, kk, ok, add_)
        ST, u = "ST%d" % t, A(P, 128, 128 + w)
        tt(A("PM", c0, c1), IND(A("PF", 1024 * h, 1024 * h + 1024), A("LK", l0, l1)), A(ST, 128 + c0, 128 + c1), mn)
        mm([(u, A("ONE32", p=1), A("CR", 0, w, p=1), True, False), (u, A("WM"), A("W255"), False, False)])
        blocks(P, 128, A("NWM"), lambda a, b: A(ST, a, b), 128 + c0, False)
        blocks(P, 128, A("WM"), lambda a, b: A("PM", a, b), c0, True)
        if not last:
            cn = A(zs[zturn[0] % 3], 0, 1)
            if h == halves[1]:
                mm([(cn, A("ONE32", p=1), A("CR", w, w + 1, p=1), True, False)]
                   + [(cn, A("ONE"), A("OK", c, c + 1), False, False) for c in range(4 - l0, 8 - l0)])
                mm([(cn, A("ONE"), A("OK", c, c + 1), False, c == l1 - 1) for c in range(l0, l1)])
                act(A("QA", 0, 1), cn, scale=1.0 / (256 * OKV), bias=24 + QB - (6144 - 15.5) / 256)
                act(A("BC", 0, 1), cn, scale=-1.0 / (256 * OKV), bias=A("QA", 0, 1))
                if cfg["ar"] == "V":
                    ts(A("AR", p=1), A("ONE", 0, 64, p=1), A("BC", 0, 1, p=1), mul, -QB, add_)
                else:
                    act(A("AR", p=1), A("ONE", 0, 64, p=1), scale=A("BC", 0, 1, p=1), bias=-QB)
        us = [A(x, w * h + UW - 1, w * h + w, UW) for x in ("U1", "U2", "U3")]
        for x, y in (("U1", "H1"), ("U2", "H2"), ("U3", "H3")):
            scan(A(x, w * h, w * h + w), A(y), u, add_, mn)
        tt(A("LU", l0, l1), us[0], us[1], sub)
        tt(A("LS", 8 + l0, 8 + l1), us[0], us[2], sub)
        dst = N - (V - 1) if last else 1
        tq, to = A("TT%d" % t, c0, c1), A("TO%d" % t, c0, c1)
        if last:
            act(A("T32", c0, c1), tq)
            tq = A("T32", c0, c1)
        tt(to, IND(A("MW", 16, 544), lm), A("DL", c0, c1), mul)
        s1 = send(A("FT" if last else "TT%d" % (t + 1), c0, c1), [tq, to], dst, after=[prev])
        nl, no = A("NL%d" % t, c0, c1), A("NO%d" % t, c0, c1)
        keep = nl
        if last:
            keep = A("LR", c0, c1)
            act(keep, nl, bias=-NOFF)
        if cfg["nmask"][h] == "V":
            tt(A("GL", c0, c1), IND(A("C", 0, 512), A("LU", l0, l1)), nl, sub)
            tt(no, IND(A("MW", 0, 528), lm), A("GL", c0, c1), mul)
        else:
            act(A("MG", c0, c1), IND(A("MW", 0, 528), lm))
            tt(A("NO%d" % t, 128 + c0, 128 + c1), IND(A("MN"), lm), keep, mul)
            keep = A("NO%d" % t, 128 + c0, 128 + c1)
            tt(no, IND(A("CO" if last else "C", 0, 512), A("LU", l0, l1)), A("MG", c0, c1), mul)
        s2 = send(A("FL" if last else "NL%d" % (t + 1), c0, c1), [keep, no], dst, after=[s1])
        if last:
            dma("Y", D("yt", c0, c1), A("FT", c0, c1))
            dma("YS"[h == halves[1]], D("yl", c0, c1), A("FL", c0, c1))
        return s2

    def records(t, h):
        c0, c1, l0, l1 = 64 * h, 64 * h + 64, 8 + 4 * h, 12 + 4 * h
        n0, lk, av = 1024 * h, A("LK", 4 * h, 4 * h + 4), A("J%d" % h, 256, 320)
        fk, bk = A("FK", c0, c1), A("FB", c0, c1)
        act(fk, IND(A("F", n0, n0 + 1024), lk))
        act(bk, IND(A("B", n0, n0 + 1024), lk))
        mm([(av, A("ID"), fk, True, False), (av, A("ID"), bk, False, True)])
        act(A("AV", c0, c1), av, bias=135.75, scale=0.5)
        tt(IND(A("X", xwin[h], n0 + 1024 + ROT), A("LS", l0, l1)), A("AV", c0, c1), A("M128", c0, c1), add_)
        if t == V - 1:
            dma("YS"[h], D("yx", n0, n0 + 1024), A("X", n0 + ROT, n0 + 1024 + ROT), 600.0)
        elif h == 1:
            copy(cfg["over"], A("X", 0, ROT), A("X", 2048, 2048 + ROT))

    def controls(t):
        last = t == V - 1
        tt(A("BX"), A("OK"), A("B0"), add_)
        ts(A("U4"), A("U1", UW - 1, 2 * w, UW), 3, band)
        tt(A("LS", 0, 8), A("U4"), A("BX"), add_)
        cp(IND(A("CO" if last else "C"), A("LS", 0, 8)), A("LR" if last else "NL%d" % t))
        if last:
            dma("Y", D("yc"), A("CO", 0, 512), 600.0)

    for t in range(V):
        now[0] = t
        zturn[0] = 0
        for h in halves:
            if cfg["split"][h]:
                now[1] = "a%d" % h
                index(t, h, 0, 1)
                now[1] = "i%d" % h
                index(t, h, 1, 3)
            else:
                now[1] = "i%d" % h
                index(t, h, 0, 3)
        now[1] = "c"
        if t == V - 1:
            act(A("CO", 0, 512), A("C", 0, 512), bias=-NOFF)
        for q in range(len(chunks)):
            now[1] = "b%d" % q
            big(t, q)
        for h in halves:
            now[1] = "p%d" % h
            last_send = post(t, h, last_send)
            now[1] = "r%d" % h
            records(t, h)
        now[1] = "c"
        if t + 2 < V:
            last_send = send(A("ST%d" % (t + 2)), [A("ST0")], t + 2, 1500.0, after=[last_send])
        controls(t)
    return ops


def label2(o):
    def short(x):
        x = x[2] if x[0] == "I" else x
        return x[1][:2] if x[1][:2] in ("NL", "TT", "ST", "NO", "TO") else x[1]
    if o["call"] == "mm":
        return "m" + short(o["args"][-1][2])
    return short(o["args"][0]) + ("s" if o["args"][0][0] == "I" else "")


def names(ops):
    seen, out = {}, []
    for o in ops:
        l = o["sec"] + "." + label2(o)
        seen[o["t"], l] = seen.get((o["t"], l), 0) + 1
        out.append(l + ("" if seen[o["t"], l] == 1 else "#%d" % seen[o["t"], l]))
    return out


def follow(ops, cfg, order):
    rank = {}
    for k, w in enumerate(order):
        rank[w.lstrip("+-")] = k + len(order) * (w.count("-") - w.count("+"))
    key, last = [], 0
    for o, l in zip(ops, names(ops)):
        last = rank.get(l, last)
        key.append(max(o["t"], 0) * len(order) + last)
    succ = [[] for _ in ops]
    left = [len(o["deps"] | o["order"]) for o in ops]
    for i, o in enumerate(ops):
        for j in o["deps"] | o["order"]:
            succ[j].append(i)
    ready = [i for i in range(len(ops)) if not left[i]]
    queue, free = {e: [] for e in "VSPGY"}, {e: 0.0 for e in "VSPGY"}
    start, done = [0.0] * len(ops), [0.0] * len(ops)
    while ready:
        i = min(ready, key=lambda k: (key[k], k))
        ready.remove(i)
        o = ops[i]
        start[i] = max([free[o["eng"]]] + [done[j] + cfg["lat"] for j in o["deps"]])
        free[o["eng"]] = start[i] + o["dur"]
        done[i] = free[o["eng"]] + o["lat"]
        queue[o["eng"]].append(i)
        for k in succ[i]:
            left[k] -= 1
            if not left[k]:
                ready.append(k)
    return queue, start, done


def plan_waits(ops, queue, start):
    mark = {}
    for e, q in queue.items():
        c = 0
        for i in q:
            o = ops[i]
            if o["kind"] == "c":
                c += 1
                mark[i] = ("e" + e, c)
            else:
                mark[i] = (o["sem"], 1)
    know = {e: {} for e in queue}
    seen, waits = {}, {}
    pos = {i: k for q in queue.values() for k, i in enumerate(q)}
    for i in sorted(range(len(ops)), key=lambda k: (start[k], pos[k])):
        o = ops[i]
        kn = know[o["eng"]]
        w = {}
        for j in sorted(o["deps"], key=lambda k: -start[k]):
            s, c = mark[j]
            if kn.get(s, 0) >= c:
                continue
            w[s] = max(w.get(s, 0), c)
            kn[s] = c
            if ops[j]["kind"] != "r":
                for s2, c2 in seen[j].items():
                    if kn.get(s2, 0) < c2:
                        kn[s2] = c2
        seen[i] = dict(kn)
        waits[i] = w
    total = {}
    for s, c in mark.values():
        total[s] = max(total.get(s, 0), c)
    rest = [(s, c) for s, c in total.items() if not any(waits[i].get(s, 0) >= c for i in waits)]
    return mark, waits, rest


ORDER = "s.X".split()
ORDER6 = ORDER = """
s.THF -r0.yx s.ST#5 s.ST#4 -p1.yl -c.yc i1.VI a1.VM i0.mST ++++++++++++++++++++b2.mSB b2.mPF i0.mST#2 b3.AZ s.E#2 i0.mTT -r0.LSs s.mONE a1.OFF i1.VM s.PL#2 b1.mE b0.mE i0.mTT#2 b5.B b1.mSB b1.F s.WM i1.OFF b5.F b0.F i0.QQ s.mTHF#2 b1.PF s.H1#2 s.mCR#2 b0.PF s.mTHF s.R0 s.mCR b2.mE i0.mQQ b0.SB s.SELP#2 b1.B -p0.yl b1.mPF b3.mPF s.H3 -p0.yt i0.mAR#2 b0.mPF b2.F -c.ST +b0.mSB s.COL#9 p1.MG b5.mE b3.mTHE b2.mMZ p0.LR#2 p0.LR ++i1.mQQ -c.BX s.NWM b2.B i0.VI s.THS#2 b1.SB i0.VI#2 b2.SB s.HA#3 s.HA#2 s.H2 s.M128 s.THS s.THE b2.PF b0.AZ b0.mTHE -c.LS +b4.F i0.VM b1.AZ s.H3#2 s.THK s.W255 b2.AZ i0.OFF s.H2#2 s.MW b0.mMZ b0.MZ b1.MZ b3.F s.R0#3 b1.mMZ b2.MZ s.H2#3 s.R0#2 s.R0#4 b3.PF b4.PF p1.mW255 p1.KEY s.MW#3 p1.mPM p1.DM b3.SB p1.OK p1.LK b5.mPF +b5.mSB p1.KK b4.SB p1.LM p1.PM +b3.B p1.mST b5.SB p1.TO b5.AZ b5.PF s.C c.CO +s.ONE s.MN ++b3.mSB r1.AV +a1.mST s.MW#2 -c.LSs p1.U1 +s.CI p1.TT +s.MK +s.ONE32 p0.mOK p1.FT p1.U2 s.MN#2 s.CR#2 b4.mMZ ++b5.mMZ +s.G1 b3.MZ +s.PF +s.WI +s.ABI +s.EP +b4.mSB +s.PI +s.ABI#2 b4.MZ +s.ST p1.LU +s.T3B +s.SBB +s.SA +s.COL +s.PI#4 +s.COL#2 +s.PI#2 +s.mSA p0.TT +s.G2 p0.mPM b3.mMZ +s.SD2 +s.TI +s.LI +s.SP +s.mSA#2 +s.IO +s.THI +s.X#2 p1.NL p1.NO +s.X b5.MZ +s.COL#3 +s.PI#3 +s.T3A +s.TA +b4.B p0.QA +s.B1 r1.mFB +a1.mTT#2 p1.NO#2 p0.mST +s.MK#2 +s.TB +s.N64 i0.DL s.H3#3 r1.FB +s.TA#2 +s.COL#6 p0.DM +s.TB#2 +s.PI#5 +s.SBB#2 r0.FK p0.KEY +s.ID p1.yt r1.FK +i1.mAR p1.FL s.H3#4 r0.FB +s.SA#2 s.BX p0.AR +s.COL#4 p0.OK +s.T3A#2 +b4.mE p0.KK +b3.mE p0.LK +s.ST#2 +s.SD +s.TT +s.NL s.Q64 p0.mOK#2 p1.U3 p0.LM p0.PM +s.IQ p1.LS p0.NL p0.TO p0.U1 r1.LSs p0.mW255 p0.U2 p0.NO +b4.mPF +s.EI +s.COL#7 +a1.QQ p0.BC p0.LU +s.ID32 p0.MG c.U4 +i1.DL p0.FT p0.U3 +a1.mTT +i1.mST +a1.mST#2 +p1.LR r0.mFB +s.OH#2 +s.CR +i1.QQ +s.EI#2 r0.AV r1.X +s.COL#5 +s.H1 +s.PL +s.NID +s.SD2#2 +s.COL#8 p0.FL +a1.mQQ +s.S8 +b4.AZ p0.NO#2 +s.WR +i1.mTT +s.HA +s.OH +s.E +a1.VI r1.yx +s.COL#10 p0.LS +b0.B +s.IO#2 +s.ST#3 +i0.mAR +s.SELP +s.mNID +p1.LR#2
""".split()
CFG.update(ar="V", over="S", chunks=[(1, 0, 7, 'V', 'S', 'V'), (1, 7, 12, 'S', 'S', 'V'), (1, 12, 16, 'S', 'V', 'V'), (0, 0, 7, 'V', 'S', 'V'), (0, 7, 13, 'S', 'S', 'V'), (0, 13, 16, 'S', 'S', 'V')])
OPS = build_ops(CFG)
QUEUE, START, DONE = follow(OPS, CFG, ORDER)
MARK, WAITS, REST = plan_waits(OPS, QUEUE, START)
KIND = {o["sem"]: o["kind"] for o in OPS if o["sem"]}
SEMAPHORES = ["eV", "eS", "eP", "eG", "sent"] + list(KIND)


def rank_program(g, core, T, topo):
    rank = T.rank_of(core)
    if rank is None:
        return
    engs = {"V": g.vector, "S": g.scalar, "P": g.tensor, "G": g, "Y": g.sync}
    arrive = {}
    for o in OPS:
        if o["kind"] == "r":
            arrive[o["sem"]] = len(topo.engines(T.cores[(rank - o["dst"]) % N], core))

    def count(s, c):
        return c if s not in KIND else 16 if KIND[s] == "d" else arrive[s]

    sent = 0
    for e, q in QUEUE.items():
        eng = engs[e]
        for i in q:
            o = OPS[i]
            for s, c in WAITS[i].items():
                eng.wait_ge(T.sem[s], count(s, c))
            call = o["call"]
            if call == "remote":
                d = T.cores[(rank + o["dst"]) % N]
                rid, pid = topo.addr(d, core)
                a = [resolve(T, x) for x in o["args"]]
                if len(a) == 2:
                    g.remote_dma(a[0], a[1], T.sem[o["sem"]], T.sem.sent, pid, rid, topo.mask(core, d))
                else:
                    g.remote_dma_fused([RemoteDMATransfer(dst_ids=[DstId(rid=rid, pnc=pid)], dma_engine_mask=topo.mask(core, d),
                                                          remote_sem=T.sem[o["sem"]], srcs=a[1:], dsts=a[:1], alu_op=1)],
                                       local_sem=T.sem.sent)
                sent += len(topo.engines(core, d))
                continue
            if call == "mm":
                for m in o["args"]:
                    ins = eng.matmul(resolve(T, m[0]), resolve(T, m[1]), resolve(T, m[2]), m[3], m[4])
            else:
                a = [resolve(T, x) for x in o["args"]]
                kw = {k: resolve(T, x) for k, x in o["kw"].items()}
                if call == "tensor_scalar": ins = eng.tensor_scalar(*a)
                elif call == "tensor_copy": ins = eng.tensor_copy(*a)
                elif call == "tensor_tensor": ins = eng.tensor_tensor(*a)
                elif call == "tensor_tensor_scan": ins = eng.tensor_tensor_scan(*a)
                elif call == "memset": ins = eng.memset(*a)
                elif call == "activation": ins = eng.activation(*a, **kw)
                elif call == "iota": ins = eng.iota(*a, **kw)
                else: ins = eng.dma_start(*a)
            s = MARK[i][0]
            ins.then_inc(T.sem[s], 16 if o["kind"] == "d" else 1)
    g.wait_ge(T.sem.sent, sent)
    for s, c in REST:
        g.wait_ge(T.sem[s], count(s, c))
